import numpy as np, ml_dtypes
CORES = [8,136,40,168]
N = 4
BF = ml_dtypes.bfloat16
def gentries(a):
    return np.ascontiguousarray(a.reshape(8, 16, -1).transpose(0, 2, 1)).reshape(8, -1)
def gtable(e):
    e = np.asarray(e); return np.ascontiguousarray(e.reshape(8, -1, 16).transpose(0, 2, 1)).reshape(128, -1).astype(np.int32)
W, P, V, EPS = 2048, 256, 4, 2
S = W // P
AG, LO, WIN, MAJ = 12, 4, 12, 9
def pick(rng, cl, want):
    out = np.zeros(want.shape, np.int64); z = rng.random(want.shape)
    for q in range(N):
        for g in range(8):
            o = np.argsort(cl[q, g], kind="stable"); lo = np.searchsorted(cl[q, g][o], np.arange(6)); n = np.maximum(lo[1:] - lo[:-1], 1); v = want[q, g]
            out[q, g] = o[np.minimum(lo[v] + (z[q, g] * n[v]).astype(np.int64), W - 1)]
    return out
def turned(a):
    return np.ascontiguousarray(np.swapaxes(a, 2, 3))
def pack(X, L, R, y, w):
    return {"xc": np.ascontiguousarray(X.reshape(N, 128, W)).astype(np.float32).astype(BF), "lsr": np.ascontiguousarray(L.reshape(N, 128, W)).astype(np.int32),
            "jur": np.stack([gtable(a.reshape(8, -1)) for a in R]), "own": np.ascontiguousarray(y.reshape(N, 128, P)).astype(np.float32).astype(BF), "wgt": w.reshape(N, 128, 1).astype(np.int32)}
def world(rng):
    pr = rng.integers(0, 16, (8, 4, 16)); gi = np.arange(8).reshape(1, 8, 1)
    z = np.where(rng.random((N, 8, W)) < 0.7, rng.random((1, 8, W)), rng.random((N, 8, W))); m = (0.45 + 0.04 * rng.permutation(8)).reshape(1, 8, 1)
    cl = (z >= m).astype(np.int64) + (z >= m + 0.15) + (z >= m + 0.2)
    p = pr[gi, cl]
    X = np.clip(p + rng.integers(-EPS, EPS + 1, p.shape), 0, 15)
    X = np.where(rng.random(p.shape) < rng.choice(np.array([0.04, 0.12, 0.3]), (N, 8, W, 1)), rng.integers(0, 16, p.shape), X)
    tr = (5 * np.arange(16) + rng.integers(0, 16, (N, 8, W, 1))) & 15
    X = np.where(cl[..., None] == 3, np.where(tr < 5 + rng.integers(0, 2, (N, 8, W, 1)), (p + 8) & 15, p), X)
    yc = rng.choice(4, (N, 8, P), p=[0.5, 0.25, 0.1, 0.15]); yp = pr[gi, yc]
    y = np.where(rng.random(yp.shape) < rng.choice(np.array([0.0, 0.1]), (N, 8, P, 1)), rng.integers(0, 16, yp.shape), yp)
    bias = rng.choice(np.array([0.0, 0.2, 0.5, 1.0]), (N, 8, P, 1)); want = np.repeat(yc[..., None], 16, axis=3)
    R = np.where(rng.random((N, 8, P, 16)) < bias, pick(rng, cl, want), rng.integers(0, W, (N, 8, P, 16)))
    return turned(X), rng.integers(0, W, (N, 8, 16, W)), R, turned(y), rng.integers(0, W, (N, 8, 16)), pr
def flood(rng, X, R, y):
    b = np.arange(16); h = np.where(b < 8, 15, 0); a = 15 * (b & 1)
    X[1, :, :, 0] = 0; X[1, :, :, W - 1] = 15; X[2, :, :, 0] = 15; X[2, :, :, W - 1] = h.reshape(1, 16)
    y[1] = h.reshape(1, 16, 1); y[2] = a.reshape(1, 16, 1); y[2, 7, :, P - 1] = h
    R[1] = (W - 1) * (np.argsort(rng.random((8, P, 16)), axis=2) < 5); R[2] = (W - 1) * rng.integers(0, 2, (8, P, 16)); R[2, 7, P - 1] = W - 1
def setup_inputs(rng):
    return pack(*world(rng)[:5])
def setup_inputs_spread(rng):
    X = (16 * rng.random((N, 8, 1, W)) ** 3 * rng.random((N, 8, 16, W))).astype(np.int64)
    y = (16 * rng.random((N, 8, 1, P)) ** 3 * rng.random((N, 8, 16, P))).astype(np.int64)
    e = 1 + 0.25 * rng.permutation(8); lw = W.bit_length() - 1
    L = (W * rng.random((N, 8, 16, W)) ** e.reshape(1, 8, 1, 1)).astype(np.int64)
    R = (W * rng.random((N, 8, P, 16)) ** e[::-1].reshape(1, 8, 1, 1)).astype(np.int64)
    w = np.minimum(np.exp2(lw * rng.random((N, 8, 16))).astype(np.int64), W - 1)
    return pack(X, L, R, y, w)
def setup_inputs_ends(rng):
    kind = rng.integers(0, 3, (N, 8, 1, W)); X = np.where(kind == 0, 0, np.where(kind == 1, 15, 15 * rng.integers(0, 2, (N, 8, 16, W))))
    L = (W - 1) * rng.integers(0, 2, (N, 8, 16, W)); flip = rng.integers(0, 2, (N, 8, 1)); X[..., 0] = 15 * flip; X[..., W - 1] = 15 - 15 * flip
    nf = rng.choice(np.array([0, 0, 1, 4, 5, 8]), (N, 8, 1, P)); base = rng.integers(0, 2, (N, 8, 1, P))
    y = 15 * np.where(np.argsort(rng.random((N, 8, 16, P)), axis=2) < nf, 1 - base, base)
    y[..., 0] = 15; y[..., 1] = 0; y[..., P - 1] = 15
    m = rng.choice(np.array([0, 4, 5, 11, 12, 16]), (N, 8, P, 1)); R = (W - 1) * (np.argsort(rng.random((N, 8, P, 16)), axis=3) < m)
    w = (W - 1) * rng.integers(0, 2, (N, 8, 16)); w[0, 0] = 0; w[N - 1, 7] = W - 1
    X[N - 1, 7, :, 0] = 0; X[N - 1, 7, :, W - 1] = 15; R[N - 1, 7, P - 1] = W - 1; R[N - 1, 7, 0] = W - 1
    h = P // 2
    for q, g in ((0, 2), (N - 1, 6)):
        w[q, g] = 0; w[q, g, 13:] = W - 1; X[q, g, :, W - 1] = 0; X[q, g, :, 0] = 15; L[q, g, :, W - 1] = 0
        y[q, g, :, h:] = 0; y[q, g, 15, h:] = 1; y[q, g, 13:15, h + h // 2:] = 15; R[q, g, h:] = W - 1; R[q, g, h::2, :4] = 0
    for q, g in ((0, 5), (N - 1, 7)):
        top = X[q, g, :, W - 1].copy(); X[q, g, :, W - 2] = top; X[q, g, 0, W - 2] = abs(int(top[0]) - 1); w[q, g, 0] = W - 1
        s = P - P // 4; i = np.arange(s, P - 1).reshape(-1, 1)
        y[q, g, :, s:P - 1] = (15 - top).reshape(16, 1); R[q, g, s:P - 1] = W - 1 - (np.arange(16) > i % 15).astype(np.int64)
    L[N - 1, 5, :, W - S:] = W - 1
    flood(rng, X, R, y)
    return pack(X, L, R, y, w)
def setup_inputs_corners(rng):
    b = np.arange(16); bb = np.where(b < 3, b, b - 1); pr = rng.integers(4, 12, (8, 16)); p = pr.reshape(1, 8, 1, 16)
    cl = rng.integers(0, 5, (N, 8, W)); c = cl[..., None]; tr = (4 * bb + rng.integers(0, 15, (N, 8, W, 1))) % 15
    off = ((b != 3) & (tr < np.where(c == 1, 5, np.where((c == 0) | (c == 2), 4, 0)))) | ((c == 2) & (b == 3))
    sg = np.where(b == 3, 1, 2 * rng.integers(0, 2, (N, 8, W, 16)) - 1); step = np.where(off, EPS + 1, np.where(c < 2, EPS, 0))
    X = np.where(c == 3, (p + 8) & 15, p + sg * step)
    na = rng.choice(np.array([0, 4, 5, 11, 12, 16]), (N, 8, P, 1)); kind = rng.integers(0, 5, (N, 8, P, 1)); o = np.argsort(rng.random((N, 8, P, 16)), axis=3)
    dis = np.where(kind < 3, kind + 1, np.where(o - na < np.where(kind == 3, 9, 8), 2, 1))
    R = pick(rng, cl, np.where(o < na, np.where((o & 1) == 1, 0, 4), dis)); h = P // 4
    R[:, 5, :h] = S * np.arange(h).reshape(1, h, 1) + (b & (S - 1)); R[:, 5, h:2 * h] = (W - 1) * rng.integers(0, 2, (N, h, 16))
    y = np.repeat(pr.reshape(1, 8, 16, 1), P, axis=3); y = np.repeat(y, N, axis=0); y[..., 7::8] = (y[..., 7::8] + 8) & 15
    way = rng.integers(0, 4, (N, 8, 16, W)); L = np.where(way == 0, np.arange(W), np.where(way == 1, 0, np.where(way == 2, W - 1, rng.integers(0, W, (N, 8, 16, W)))))
    L[:, 2] = np.arange(W); L[:, 3] = rng.integers(0, W, (N, 16, W)); L[:, 6] = rng.integers(0, W, (N, 16, W))
    w = rng.integers(0, W, (N, 8, 16)); w[:, 0] = 0; w[:, 1] = W - 1; w[:, 2] = 1; w[:, 3] = 0; w[:, 3, 15] = W - 1; w[:, 4] = 0; w[:, 4, 0] = 1
    return pack(turned(X), L, R, y, w)
def setup_inputs_crowd(rng):
    X, L, R, y, w, pr = world(rng); bc = rng.integers(1, W - 1, 8); b2 = rng.integers(1, W - 1, 8)
    for g in range(8):
        for q in range(N):
            X[q, g, :, b2[g]] = pr[g, (q >> 1) & 1]; X[q, g, :, bc[g]] = pr[g, q & 1]
        if (g & 3) < 2:
            one = np.argsort(rng.random((N, P, 16)), axis=2) == 0
            R[:, g] = np.where(one, R[:, g], bc[g]) if (g & 3) == 1 else bc[g]
        elif (g & 3) == 2: R[:, g] = rng.choice(np.array([0, bc[g], W - 1]), (N, P, 16))
        L[:, g] = rng.choice(np.array([bc[g], b2[g], 0, W - 1]), (N, 16, W)) if (g & 1) == 1 else b2[g]
    flood(rng, X, R, y)
    return pack(X, L, R, y, w)
def setup_inputs_calm(rng):
    pr = rng.integers(0, 16, (8, 16)); p = pr.reshape(1, 8, 16, 1)
    cl = (rng.random((8, W)) < (0.3 + 0.05 * rng.permutation(8)).reshape(8, 1)).astype(np.int64); cl[:, 1] = 0; cl[:, W - 1] = 1
    X = np.minimum(np.where(cl.reshape(1, 8, 1, W) == 1, (p + 8) & 15, p) + rng.integers(0, 2, (N, 8, 16, W)), 15)
    X[..., 0::2] = rng.integers(0, 16, (N, 8, 16, W // 2))
    y = np.minimum(p + rng.integers(0, 2, (N, 8, 16, P)), 15); w = 2 * rng.integers(0, W // 2, (N, 8, 16))
    o = np.argsort(rng.random((N, 8, P)), axis=2); c = np.where(o < P // 4, 5, rng.integers(6, 17, (N, 8, P)))
    few = np.array([0, 2, 1, 3])[(np.arange(N) + int(rng.integers(0, 4))) & 3]
    for q in range(N):
        for g in rng.permutation(8)[:int(few[q])]:
            c[q, g, np.argmax(o[q, g])] = rng.integers(0, 5)
    near = np.argsort(rng.random((N, 8, P, 16)), axis=3) < c[..., None]
    L = np.zeros((N, 8, 16, W), np.int64); R = np.zeros((N, 8, P, 16), np.int64); odd = np.arange(1, W, 2)
    for g in range(8):
        good, far = odd[cl[g, odd] == 0], odd[cl[g, odd] == 1]
        L[:, g] = np.where(cl[g] == 0, good[rng.integers(0, len(good), (N, 16, W))], far[rng.integers(0, len(far), (N, 16, W))])
        R[:, g] = np.where(near[:, g], good[rng.integers(0, len(good), (N, P, 16))], far[rng.integers(0, len(far), (N, P, 16))])
    return pack(X, L, R, y, w)
def check_inputs(d):
    bad = []
    for k, hi in (("xc", 15), ("lsr", W - 1), ("jur", W - 1), ("own", 15), ("wgt", W - 1)):
        v = np.asarray(d[k]).astype(np.float64)
        if not (np.min(v) >= 0 and np.max(v) <= hi): bad.append("range of " + k)
        elif np.any(v != np.floor(v)): bad.append("whole numbers of " + k)
    return bad
def reference(xc, lsr, jur, own, wgt):
    X = xc.astype(np.float32).astype(np.int32).reshape(N, 8, 16, W); L = lsr.astype(np.int64).reshape(N, 8, 16, W)
    R = np.stack([gentries(a) for a in jur]).astype(np.int64).reshape(N, 8, P, 16)
    y = own.astype(np.float32).astype(np.int32).reshape(N, 8, 16, P); w = wgt.astype(np.int64).reshape(N, 8, 16, 1)
    A = np.zeros(N, np.int64); k = np.arange(16); g3 = np.arange(8).reshape(8, 1, 1); g2 = np.arange(8).reshape(8, 1); i2 = np.arange(P).reshape(1, P); b3 = k.reshape(1, 16, 1)
    for t in range(V):
        for r in range(N):
            q = (r + t) % N; old = R[r].copy()
            x = np.take_along_axis(X[q], old.reshape(8, 1, 16 * P), 2).reshape(8, 16, P, 16)
            n = L[q][g3, (k + t) & 15, old]
            z = np.take_along_axis(X[q], n.reshape(8, 1, 16 * P), 2).reshape(8, 16, P, 16)
            v = y[r]; d = np.abs(x - v[..., None])
            a = np.sum(d <= EPS, axis=1) >= AG; c = np.sum(a, axis=2)
            lost = c <= LO + (A[q] & 1)
            rho = np.argmax(np.sum(d > EPS, axis=3) >= MAJ, axis=1)
            e = np.argmin(np.where(a, 1000, np.sum(d, axis=1)), axis=2)
            v = np.where(lost[:, None, :] & (b3 == rho[:, None, :]), x[g2, rho, i2, e][:, None, :], v)
            a = np.sum(np.abs(x - v[..., None]) <= EPS, axis=1) >= AG; c = np.sum(a, axis=2)[..., None]
            u = np.sum(w[q] * v, axis=1) & (W - 1)
            za = np.sum(np.abs(z - v[..., None]) <= EPS, axis=1) >= AG
            far = (((old * u[..., None]) >> 5) + old + 37 * k) & (W - 1)
            new = np.where((c >= WIN) & a, np.where(za, n, far), np.where((c > LO) & (c < WIN) & ~a, n, old))
            col = (S * i2 + (u & (S - 1)))[:, None, :]
            if t < V - 1: X[q][g3, b3, col] = v
            L[q][g3, b3, col] = new.transpose(0, 2, 1)
            R[r] = new; y[r] = v; A[q] = np.sum(lost)
    return {"yj": np.ascontiguousarray(R.transpose(0, 1, 3, 2)).reshape(N, 128, P).astype(np.float32), "yo": y.reshape(N, 128, P).astype(np.float32).astype(BF),
            "yz": np.sum(L * (k + 1).reshape(1, 1, 16, 1), axis=2).astype(np.float32)}

@@ -1,0 +1,584 @@
+from concourse.mybir import AluOpType as OP, ActivationFunctionType as AF
+
+V = 4
+H = 128
+F32, BF, F16, I32, U16 = "float32", "bfloat16", "float16", "int32", "uint16"
+
+
+def _sb(n, d):
+    return ("sbuf", [128, n], d)
+
+
+SCRATCH = {
+    "xin": _sb(2048, BF), "lin": _sb(2048, I32), "jin": _sb(256, I32), "win": _sb(8, I32), "tab": _sb(2048, F32),
+    "hx": _sb(2048, BF), "yzt": _sb(2048, F32),
+    "yi": _sb(256 * 5, BF), "ui": _sb(256 * 4, U16), "yq": _sb(256 * 4, BF), "uq": _sb(256 * 3, U16),
+    "rq": _sb(256, F32), "ri": _sb(256, F32),
+    "gg": _sb(4096, F32), "zz": _sb(4096, BF), "d": _sb(4096, BF), "fx": _sb(4096, BF), "ad": _sb(4096, BF),
+    "fz": _sb(4096, BF), "az": _sb(4096, BF), "wp": _sb(1024, F32), "tp": _sb(1024, F32),
+    "dif": _sb(128, F32), "gm": _sb(128, F32), "gj": _sb(128, F32), "g4": _sb(32, F32), "zc": _sb(144, F32),
+    "pi": _sb(8, I32), "pj": _sb(8, I32), "pf": _sb(32, F32),
+    "i32": _sb(128, F32), "ib": _sb(128, BF), "ih": _sb(128, F16), "nih": _sb(128, F16), "nib": _sb(128, BF), "bo": _sb(128, BF),
+    "i4k": _sb(128, BF), "n4k": _sb(128, BF), "ibig": _sb(128, BF), "i16": _sb(128, BF), "tri": _sb(128, BF), "tmp": _sb(128, BF),
+    "w1": _sb(128, BF), "w2": _sb(128, BF), "zs": _sb(144, BF), "zw": _sb(144, BF), "g8s": _sb(8, BF),
+    "g8": _sb(8, BF), "wh": _sb(128, BF), "wl": _sb(128, BF), "wz": _sb(128, F16), "wz32": _sb(128, F32), "wz4": _sb(128, BF),
+    "nwz4": _sb(128, BF), "c128": _sb(512, BF), "c160": _sb(128, BF), "cu": _sb(128, F16), "c32": _sb(128, F16),
+    "pk": _sb(144, BF), "fw": _sb(128, BF), "sj": _sb(32, F32),
+    "ini": _sb(128, BF), "rst": _sb(128, F32), "o16": _sb(128, F32), "ends": _sb(8, U16), "endi": _sb(8, I32),
+    "base": _sb(16, I32), "wcol": _sb(16, F32), "wcb": _sb(16, BF),
+    "r16": _sb(256, F16), "n32": _sb(256, F32), "nr": _sb(256, BF), "nu": _sb(256, U16), "n16": _sb(256, F16),
+    "a": _sb(256, BF), "pc": _sb(256, BF), "nl": _sb(256, BF), "bad": _sb(256, BF), "m": _sb(256, BF), "fo": _sb(256, BF), "fn": _sb(256, BF),
+    "ra": _sb(256, F32), "dr": _sb(256, BF), "mins": _sb(256, F32), "rb": _sb(256, F32), "dbc": _sb(256, BF), "a2": _sb(256, BF),
+    "m1": _sb(256, F16), "wa": _sb(256, BF), "tf": _sb(256, BF), "ur": _sb(256, BF), "pp": _sb(256, F32), "pq": _sb(256, I32),
+    "far": _sb(256, I32), "fmn": _sb(256, F16), "t1": _sb(256, F16), "hh": _sb(256, F16), "h32": _sb(256, F32),
+    "cn": _sb(256, F32), "ca": _sb(16, I32), "cb": _sb(16, I32), "cc": _sb(16, I32), "col": _sb(16, U16),
+    "acc": _sb(8, F32), "ai": _sb(8, I32), "aj": _sb(8, I32), "thr": _sb(8, F32),
+}
+for _b in ("A0", "A1", "B0", "B1", "C0", "C1", "D0", "D1"):
+    SCRATCH["ps" + _b] = ("psum", [128, 512], F32)
+
+SEMAPHORES = (["cpe", "cact", "cdve", "cpool", "sent"] + ["dm%d" % i for i in range(16)]
+              + ["ar%d" % i for i in range(16)])
+
+GATH_G = [[("act", 0, 64), ("dve", 64, 128)], [("act", 0, 64), ("act", 64, 128)]]
+GATH_Z = [[("act", 0, 32), ("act", 32, 64), ("act", 64, 96), ("act", 96, 128)]] * 2
+HX_ENG = ["dve", "act", "dve", "act"]
+FZ_ACT = [(), ()]
+COST = {"cyc": 0.00100, "pec": 0.00050, "ovh": 0.06, "pov": 0.005, "lat": 0.12, "gc": 1.55, "sc": 3.8, "net": 2.5}
+MEMO = {}
+RANKING = """
+awa_1a dd0_0a pC00c awa_0a pC00b dd0_1a ddbc_1a anr_1a dd2_0a pui0a ayzt0a pB00c dfz1_0a ag0_0a az0_0a pA00a drq_0a
+dmins_0a ag0_1a pB00a az64_0a dd1_0a anr_0a dg64_0a am_0a dfz0_1a dfx2_0a az0_1a pB10a dfx2_1a pD00a pD03a dyq1a pC11d
+pA10g dd1_1a ddr_0a dd3_0a dra_0a anl_1a dhh_1a dn16_1a dfn_1a ag64_1a aad0_1a dcaa dfx0_0a dmins_1a pD10a awp_0a dm1_0a
+pA00d pD01a pC11a aad2_0a dd2_1a dfx0_1a daja an32_0a aad0_0a pC02a pD03b dd3_1a pD13a pA00c pA00b abad_1a dr16_0a
+anl_0a dt1_1a dn16_0a pB00b aa2_1a aad2_1a pC10b pA10c pD11c pB10e az32_0a pA10a ahx1a pC00a dpq_1a pA00e pC10a drb_0a
+abad_0a pA10b aa2_0a pyzp3a ahx3a ddr_1a pC01d dtp_1a pB00d pB10b drq_1a pA00g an32_1a pC01a pD02a pD12a pA10d pC10c
+dr16_1a dtp_0a aa_0a pD11a pC13a pB01a pA00f pD12b dfz2_1a awp_1a az32_1a az96_1a pyi0a pB10c pC03e az96_0a pA10e drb_1a
+pyzp1a pD12c pC11c am_1a pC01c pD00c pC01b pC11b ddbc_0a dnu_0a pB00f pC12a pC00d pyzp2a aa_1a pB11a dra_1a ayzt3a dD03a
+dpq_0a pB00e dfn_0a dthra pD02b pC03d dfz3_0a dfz0_0a pB10d pyi1a dfz2_0a pD01b pD13b dpp_1a ahx2a dD13a dtab0a dfar_1a
+dhh_0a dfo_0a pD01c dpp_0a pD10b pB12a dnu_1a dyq0a pD03d pD03c pyzp0a pD10c dfz1_1a pC03a pD13c duq0a acn_0a pB00g
+dyzt0a dcca pD00b dm1_1a dur_1a pA00h pC13d dcba pA10h pD11b pC03b pD13d daia ahx0a pC13b pD02c ayzt2a dfo_1a pB10f
+dur_0a az64_1a pC13e dtab0b ayzt1a pA10f atf_1a pA11a dfmn_1a pC13c pC10d dfar_0a atf_0a pri_0a acn_1a dt1_0a pui1a
+pC03c dyzt0b dfz3_1a dfmn_0a pB10g duq1a dcola pri_1a
+"""
+RANKING = """
+dra_1a ag0_0a dg64_0a pyzp1a pD03a dfx0_1a pD13a dhx0a pyzp0a aa_0a dd0_0a dd1_0a dd2_0a dd3_0a ahx1a ag0_1a ag64_1a
+dfx0_0a dfx2_0a dhx2a ayzt0a ayzt3a pA00b pyzp2a pD00a pB00a pA00c dd0_1a dd1_1a dd2_1a dd3_1a pD01a ahx3a pA00d aad0_0a
+pB00b aad2_0a pA10a pB03a awp_0a abad_0a pC00a pB00d ayzt2a pB00c dfx2_1a am_0a pD10a pA10b pC01a pC10a ayzt1a pD00b
+pA00a pB10a pA10c pyzp3a pC01b dtp_0a an32_0a pA00e pD02a dr16_0a pA10d anr_0a pB10b aad2_1a pB01a pB13a awp_1a pB02a
+pC01c abad_1a aad0_1a anl_0a pB12a pB10c pD11a az32_0a am_1a dra_0a az0_0a az64_0a az96_0a pA10e pB10d aa_1a dnu_0a
+pC11b pC01d dtp_1a pD12a dr16_1a ddr_0a an32_1a anr_1a anl_1a pui0a drb_0a apc_0a pC11c dfz0_0a pB11a ddbc_0a dnu_1a
+dn16_0a dD03a az0_1a az32_1a az64_1a ddr_1a dyq0a pC11d pC00b pB00e pA00f dfn_0a pC02a drb_1a pC11a dpq_0a dmins_1a
+dmins_0a pD03b ddbc_1a dfz1_0a aa2_0a pD13b dur_0a pC13e dn16_1a dD13a pD01b awa_0a dfo_1a pB00f apc_1a pC03a dyq1a
+dpp_0a pC10b az96_1a pC03b pD00c pD02c pB10e pA00g pA10f dfz2_0a dfn_1a pC03c dfz3_0a pD12d dfo_0a dfar_0a dm1_0a pC12a
+pD01c pD11b pD10b dfmn_0a dfz0_1a dt1_0a pC03d dfz1_1a pC03e pD12b dur_1a aa2_1a pyi0a atf_0a dcaa pB10f pD11c pA10g
+dfz3_1a dfz2_1a pD02d pC13a pyi1a pD00d dhh_0a dpp_1a pC13b pD10c pD12c acn_0a pD03c dm1_1a dpq_1a pC13c dfar_1a drq_0a
+pD11d duq0a pC13d dfmn_1a pB00g dt1_1a awa_1a pD02b dcba atf_1a duq1a dcca pri_0a dhh_1a pD13c pri_1a pD10d drq_1a
+acn_1a pui1a dtab0a dyzt0a dtab0b dyzt0b pA11a daia dcola dthra daja pB10g
+""".strip()
+
+
+def plan(g, core, T, topo):
+    rank, n = T.rank_of(core), len(T.cores)
+    nxt = T.cores[(rank + 1) % n]
+    rid, pid = topo.addr(nxt, core)
+    mask = topo.mask(core, nxt)
+    nen = len(topo.engines(core, nxt))
+    ve, ac, pe = g.vector, g.scalar, g.tensor
+    CYC, PEC, OVH, POV, GC, SC, NET = [COST[k] for k in ("cyc", "pec", "ovh", "pov", "gc", "sc", "net")]
+    ops, visit, seen = [], [-1], {}
+
+    def op(eng, cost, reads, writes, emit, kind="c"):
+        banks = sorted(set(k[:2] for k in list(reads) + list(writes) if len(k) == 4 and k[2] == "."))
+        cls = None
+        if visit[0] >= 0 and kind != "dma":
+            name = writes[0].replace(".", "")
+            if name[:2] in ("yi", "ui", "yq", "uq") and name[2:].isdigit():
+                name = name[:2] + name[3:]
+            seen[(visit[0], eng, name)] = seen.get((visit[0], eng, name), -1) + 1
+            cls = "%s%s%s" % (eng[0], name, "abcdefghijkl"[seen[(visit[0], eng, name)]])
+        ops.append({"eng": eng, "cost": cost, "r": list(reads), "w": list(writes), "emit": emit, "kind": kind, "banks": banks,
+                    "cls": cls, "at": visit[0]})
+
+    def dve(n_el, reads, writes, emit, f=1.0, calls=1):
+        op("dve", calls * (OVH + max(64, n_el * f) * CYC), reads, writes, emit)
+
+    def act(n_el, reads, writes, emit, f=1.0):
+        op("act", OVH + max(64, n_el * f) * CYC, reads, writes, emit)
+
+    def many(emits):
+        def emit():
+            last = None
+            for e in emits:
+                last = e()
+            return last
+        return emit
+
+    def mm(reads, writes, calls):
+        op("pe", 0.03 + sum(c[5] * PEC + POV for c in calls), reads, writes,
+           many([(lambda c=c: pe.matmul(c[0], c[1], c[2], c[3], c[4])) for c in calls]))
+
+    def group(out, terms, start=True, cyc=128, stop=True):
+        return [(out, w, x, start and j == 0, stop and j == len(terms) - 1, cyc) for j, (w, x) in enumerate(terms)]
+
+    def ts(out, in0, s1, s2, o0, o1=None):
+        if o1 is None:
+            return lambda: ve.tensor_scalar(out, in0, s1, None, o0)
+        return lambda: ve.tensor_scalar(out, in0, s1, s2, o0, o1)
+
+    def tt(out, in0, in1, o):
+        return lambda: ve.tensor_tensor(out, in0, in1, o)
+
+    def cp(out, in_):
+        return lambda: ve.tensor_copy(out, in_)
+
+    def af(out, in_, func, bias=0.0, scale=1.0, accum=None):
+        if accum is None:
+            return lambda: ac.activation(out, in_, func, bias, scale)
+        return lambda: ac.activation(out, in_, func, bias, scale, accum_out=accum)
+
+    def step(out, in_, at, sign=1.0, accum=None):
+        bias = -1000.0 * sign * at if isinstance(at, float) else at
+        return af(out, in_, AF.Sigmoid, bias, 1000.0 * sign, accum)
+
+    def dma(q, cost, reads, writes, out, in_, slow=False):
+        qq = {"sp": g.sync, "act": g.scalar, "pool": g}[q]
+        if slow:
+            op(q, cost, reads, writes, lambda: qq.dma_start(out, in_, allow_slow_non_contiguous=True), "dma")
+        else:
+            op(q, cost, reads, writes, lambda: qq.dma_start(out, in_), "dma")
+
+    def send(reads, writes, out, in_):
+        op("pool", NET, reads, writes, lambda sem: g.remote_dma(out, in_, sem, T.sem.sent, pid, rid, mask), "send")
+
+    def slots(b):
+        return ["%s.%d" % (b, s) for s in range(4)]
+
+    ps = {b: T["ps" + b] for b in ("A0", "A1", "B0", "B1", "C0", "C1", "D0", "D1")}
+    TAB = ["tab%d" % c for c in range(4)]
+
+    dma("sp", 2.2, [], ["lin0"], T.lin[:, 0:512], T.lsr[:, 0:512])
+    dma("act", 2.6, [], ["xin0"], T.xin[:, 0:1024], T.xc[:, 0:1024])
+    dma("sp", 3.2, [], ["lin1"], T.lin[:, 512:1024], T.lsr[:, 512:1024])
+    dma("act", 3.6, [], ["jin"], T.jin[:], T.jur[:])
+    dma("sp", 4.2, [], ["xin1"], T.xin[:, 1024:2048], T.xc[:, 1024:2048])
+    dma("act", 4.8, [], ["lin2"], T.lin[:, 1024:1536], T.lsr[:, 1024:1536])
+    dma("sp", 5.4, [], ["lin3"], T.lin[:, 1536:2048], T.lsr[:, 1536:2048])
+    dma("act", 5.6, [], ["yi00", "yi01"], T.yi[:, 0:256], T.own[:])
+    dma("pool", 3.0, [], ["win"], T.win[:, 0:1], T.wgt[:], True)
+
+    def ramp(key, out, pattern, base, mul, whole=False):
+        n_el = 1
+        for p in pattern:
+            n_el *= p[1]
+        if whole:
+            op("pool", 0.13 + 2 * n_el * CYC, [], [key], lambda: g.iota(out, pattern, base, mul))
+        else:
+            op("pool", 0.13 + 2 * n_el * CYC, [], [key],
+               lambda: g.iota(out, pattern, base, mul, allow_small_or_imprecise_dtypes=True))
+    ramp("dif", T.dif[:], [[1, 128]], 0, -1)
+    ramp("pi", T.pi[:, 0:1], [[0, 1]], 0, 1, True)
+    ramp("gm", T.gm[:], [[1, 8], [0, 16]], 0, 0)
+    ramp("zc", T.zc[:], [[1, 144]], -15, 0)
+    ramp("ini1", T.ini[:], [[0, 8], [32, 16]], -160, 0)
+    ramp("gj", T.gj[:], [[16, 8], [0, 4], [1, 4]], 0, 0)
+    ramp("g4", T.g4[:], [[1, 32]], 0, 0)
+    ramp("endi", T.endi[:], [[16, 8]], 15, 0, True)
+    ramp("base0", T.base[:], [[128, 16]], 0, 0, True)
+    for key, v in (("i4k", 4096.0), ("ib", 1.0), ("ih", 1.0), ("nih", -1.0)):
+        dve(128, ["dif"], [key], ts(T[key][:], T.dif[:], 0.0, v, OP.is_equal, OP.mult))
+    for key, v in (("nib", -1.0), ("i32", 1.0), ("n4k", -4096.0), ("ibig", 262144.0), ("i16", 16.0), ("w1", -7.0)):
+        act(128, ["ib"], [key], af(T[key][:], T.ib[:], AF.Identity, 0.0, v))
+
+    def lin(key, reads, out, in_, scale, bias=0.0, n_el=1):
+        act(n_el, reads, [key], af(out, in_, AF.Identity, bias, scale))
+    pint = lambda c: T.pj[:, c:c + 1]
+    dve(1, ["pi"], ["pj0"], ts(pint(0), T.pi[:, 0:1], 4, None, OP.arith_shift_right))
+    dve(1, ["pi"], ["pj1"], ts(pint(1), T.pi[:, 0:1], 15, None, OP.bitwise_and))
+    dve(1, ["pi"], ["pj2"], ts(pint(2), T.pi[:, 0:1], 2, None, OP.arith_shift_right))
+    dve(1, ["pi"], ["pj3"], ts(pint(3), T.pi[:, 0:1], 2, 3, OP.arith_shift_right, OP.bitwise_and))
+    dve(1, ["pi"], ["pj4"], ts(pint(4), T.pi[:, 0:1], 1, None, OP.bitwise_and))
+    dve(1, ["pi"], ["pj5"], ts(pint(5), T.pi[:, 0:1], 1, 1, OP.arith_shift_right, OP.bitwise_and))
+    PG, PK, P4, PJ, B0, B1, PG16, PM, PF, PZ, P8, PW, PV, PT, PGJ, PGJ3, PW4 = [T.pf[:, c:c + 1] for c in range(17)]
+    dve(6, ["pj%d" % j for j in range(6)], ["pf"], cp(T.pf[:, 0:6], T.pj[:, 0:6]))
+    lin("pg16", ["pf"], PG16, PG, 16.0)
+    dve(1, ["pf"], ["pm0"], ts(PW, PK, 0.0, None, OP.is_equal))
+    lin("pm", ["pm0"], PM, PW, 1000.0, -500.0)
+    lin("pfar", ["pf"], PF, PK, 37.0 * 32.0)
+    lin("pz", ["pf"], PZ, PK, 1.0, 1.0)
+    lin("p8", ["pf"], P8, PK, 8.0)
+    X0, X1, X2, X3, X4 = [T.pf[:, c:c + 1] for c in range(17, 22)]
+    lin("x0", ["pf"], X0, B0, 31.0 / 4096, 1.0 / 4096)
+    lin("x1", ["pf"], X1, B1, 1023.0, 1.0)
+    lin("pw4", ["x0", "x1"], PW4, X0, X1)
+    lin("x2", ["pf"], X2, B0, -31.0 / 32, 1.0)
+    lin("x3", ["pf"], X3, B1, -1023.0 / 1024, 1.0)
+    lin("pv", ["x2", "x3"], PV, X2, X3)
+    lin("pgj", ["pf"], PGJ, PG, 16.0, PJ)
+    lin("pgj3", ["pgj"], PGJ3, PGJ, 1.0, -3.0)
+    lin("pz4", ["pf"], PT, PK, 4096.0, 4096.0)
+    lin("npz4", ["pf"], X4, PK, -4096.0, -4096.0)
+    dve(144, ["zc", "pgj3", "pw4"], ["pk"], ts(T.pk[:], T.zc[:], PGJ3, PW4, OP.is_equal, OP.mult))
+    dve(128, ["gj", "pgj", "pv"], ["fw"], ts(T.fw[:], T.gj[:], PGJ, PV, OP.is_equal, OP.mult))
+    dve(32, ["g4", "pf"], ["sj"], ts(T.sj[:], T.g4[:], P4, None, OP.is_equal))
+    dve(16, ["base0", "p8"], ["base0"], ts(T.base[:], T.base[:], P8, None, OP.add))
+    dve(128, ["gm", "pf"], ["bo"], ts(T.bo[:], T.gm[:], PG, None, OP.is_equal))
+    dve(144, ["zc", "pg16"], ["zs"], ts(T.zs[:], T.zc[:], PG16, None, OP.is_equal))
+    lin("g8", ["bo"], T.g8[:], T.bo[:, 0:128:16], 1.0)
+    lin("g8s", ["bo"], T.g8s[:], T.bo[:, 0:128:16], 512.0)
+    dve(128, ["dif"], ["tmp"], ts(T.tmp[:], T.dif[:], 0.0, None, OP.is_gt))
+    dve(128, ["tmp", "bo"], ["tmp"], tt(T.tmp[:], T.tmp[:], T.bo[:], OP.mult))
+    dve(128, ["tmp", "ib"], ["tri"], tt(T.tri[:], T.ib[:], T.tmp[:], OP.subtract))
+    dve(8, ["ib", "tri"], ["tmp"], ts(T.tmp[:, 0:8], T.ib[:, 0:128:16], 17.0, None, OP.mult))
+    dve(8, ["tmp", "g8"], ["tri"], tt(T.tri[:, 0:128:16], T.tmp[:, 0:8], T.g8[:], OP.subtract))
+    dve(128, ["w1", "bo"], ["w1"], tt(T.w1[:], T.w1[:], T.bo[:], OP.add))
+    dve(128, ["i16", "bo"], ["w2"], tt(T.w2[:], T.i16[:], T.bo[:], OP.add))
+    dve(128, ["gm", "pf", "pz"], ["wz"], ts(T.wz[:], T.gm[:], PG, PZ, OP.is_equal, OP.mult))
+    lin("wz32", ["bo", "pz"], T.wz32[:], T.bo[:], PZ, 0.0, 128)
+    lin("wz4", ["bo", "pz4"], T.wz4[:], T.bo[:], PT, 0.0, 128)
+    lin("nwz4", ["bo", "npz4"], T.nwz4[:], T.bo[:], X4, 0.0, 128)
+    dve(8, ["endi"], ["ends"], cp(T.ends[:], T.endi[:]))
+
+    def fill(key, ap, v, n_el):
+        dve(n_el, [], [key], lambda: ve.memset(ap, v), 0.5)
+    fill("c160", T.c160[:], -160.0, 128)
+    fill("c128", T.c128[:], 128.0, 512)
+    fill("cu", T.cu[:], -1023.5, 128)
+    fill("c32", T.c32[:], 32.0, 128)
+    fill("rst", T.rst[:], -1.0e6, 256)
+    dve(8, ["rst"], ["rst"], lambda: ve.memset(T.rst[:, 0:128:16], 131072.0))
+    fill("o16", T.o16[:], 0.0625, 256)
+    fill("thr", T.thr[:, 0:1], -4500.0, 1)
+    WF, WLO, W7 = T.wcol[:, 0:1], T.wcol[:, 1:2], T.wcol[:, 2:3]
+    dve(1, ["win"], ["wf"], cp(WF, T.win[:, 0:1]))
+    dve(1, ["wf"], ["whi"], cp(T.wcb[:, 0:1], WF))
+    dve(1, ["wf", "whi"], ["wlo"], tt(WLO, WF, T.wcb[:, 0:1], OP.subtract))
+    dve(1, ["win"], ["w7i"], ts(T.win[:, 4:5], T.win[:, 0:1], 7, None, OP.bitwise_and))
+    dve(1, ["w7i"], ["w7"], cp(W7, T.win[:, 4:5]))
+    lin("wh", ["bo", "wf"], T.wh[:], T.bo[:], WF, 0.0, 128)
+    lin("wl", ["bo", "wlo"], T.wl[:], T.bo[:], WLO, 0.0, 128)
+    lin("zw", ["zs", "w7"], T.zw[:], T.zs[:], W7, 0.0, 144)
+    dve(256, ["jin"], ["ui00", "ui01"], cp(T.ui[:, 0:256], T.jin[:]))
+    for c, b in enumerate(("A0", "A1", "B0", "B1")):
+        s = slice(512 * c, 512 * c + 512)
+        mm(["i4k", "xin%d" % (c // 2)], slots(b), [(ps[b][:], T.i4k[:], T.xin[:, s], True, True, 512)])
+        dve(512, slots(b) + ["lin%d" % c], ["tab%d" % c], tt(T.tab[:, s], T.lin[:, s], ps[b][:], OP.add))
+
+    CX, CD, CM, CU, CK = 1.5 * 2 ** 37, 1.5 * 2 ** 25, 1.5 * 2 ** 26, 1.5 * 2 ** 34, 1.5 * 2 ** 28
+
+    def half(t, h):
+        last = t == V - 1
+        k_ = lambda s: "%s_%d" % (s, h)
+        c = slice(H * h, H * h + H)
+        A, B, C, D = "A%d" % h, "B%d" % h, "C%d" % h, "D%d" % h
+        sl = lambda b, s: ps[b][:, H * s:H * s + H]
+        o0 = 256 * t + H * h
+        o1 = o0 + 256
+        Y, U, YN = T.yi[:, o0:o0 + H], T.ui[:, o0:o0 + H], T.yq[:, o0:o0 + H]
+        ky, ku, kyn = "yi%d%d" % (t, h), "ui%d%d" % (t, h), "yq%d%d" % (t, h)
+        q0 = 2048 * h
+        ch = lambda buf, q, w=1: buf[:, q0 + 512 * q:q0 + 512 * (q + w)]
+        kk = lambda buf, k: buf[:, q0 + H * k:q0 + H * (k + 1)]
+        gj = lambda buf, k: buf[:, q0 + k:q0 + 2048:16]
+        wq = T.wp[:, 512 * h:512 * h + 512]
+        tq = T.tp[:, 512 * h:512 * h + 512]
+        gk = []
+        for e, i0, i1 in GATH_G[h]:
+            src = T.tab[:, 0:2048].indirect(T.ui[:, o0 + i0:o0 + i1])
+            out = T.gg[:, q0 + 16 * i0:q0 + 16 * i1]
+            gk.append(k_("g%d" % i0))
+            if e == "act":
+                act(16 * (i1 - i0), TAB + [ku], gk[-1:], af(out, src, AF.Identity), GC)
+            else:
+                dve(16 * (i1 - i0), TAB + [ku], gk[-1:], cp(out, src), GC)
+        mm(["i4k", "c160", ky], [D + ".3"], group(sl(D, 3), [(T.i4k[:], T.c160[:, 0:H]), (T.i4k[:], Y)]))
+        if last:
+            for q in (2 * h, 2 * h + 1):
+                s = slice(512 * q, 512 * q + 512)
+                if HX_ENG[q] == "act":
+                    act(512, TAB, ["hx%d" % q], af(T.hx[:, s], T.tab[:, s], AF.Identity, 128.0, 1.0 / 4096))
+                else:
+                    dve(512, TAB, ["hx%d" % q], ts(T.hx[:, s], T.tab[:, s], 1.0 / 4096, 128.0, OP.mult, OP.add))
+                mm(TAB + ["hx%d" % q, "wz4", "nwz4", "wz32", "c128"], ["yzp%d" % q] + slots(C),
+                   [(ps[C][:], T.wz4[:], T.c128[:], True, False, 512), (ps[C][:], T.nwz4[:], T.hx[:, s], False, False, 512),
+                    (ps[C][:], T.wz32[:], T.tab[:, s], False, True, 2048)])
+                act(512, slots(C), ["yzt%d" % q], af(T.yzt[:, s], ps[C][:], AF.Identity))
+        mm(["ib", "ini1"], slots(C), [(sl(C, 1), T.ib[:], T.ini[:], True, False, 128)])
+        dve(H, [ku], [k_("r16")], cp(T.r16[:, c], U), 0.5)
+        for q in range(4):
+            dve(H, gk + [D + ".3"], [k_("d%d" % q)],
+                many([tt(kk(T.d, k), gj(T.gg, k), sl(D, 3), OP.subtract) for k in range(4 * q, 4 * q + 4)]), 1.0, 4)
+            mm([k_("d%d" % q), "pk"] + slots(A), slots(A), [(ps[A][:], T.pk[:, 12 - 4 * q:140 - 4 * q], ch(T.d, q), q == 0, q == 3, 512)])
+        for q in (0, 2):
+            dk = [k_("d%d" % q), k_("d%d" % (q + 1))]
+            dve(1024, dk, [k_("fx%d" % q)], ts(ch(T.fx, q, 2), ch(T.d, q, 2), CX - 160.0 * 4096, CX, OP.add, OP.not_equal), 0.5)
+            act(1024, dk, [k_("ad%d" % q)], af(ch(T.ad, q, 2), ch(T.d, q, 2), AF.Abs, -160.0, 1.0 / 4096))
+            ks = range(4 * q, 4 * q + 8)
+            mm([k_("ad%d" % q), "g8s", C + ".1"], [C + ".1"],
+               [(ps[C][:, H + k:2 * H:16], kk(T.ad, k), T.g8s[:], False, False, 64) for k in ks])
+        act(512, slots(A), [k_("wp")], af(wq, ps[A][:], AF.Identity, -160.0 * 33825))
+        for q in range(4):
+            mm(gk + ["i32"], [B + ".0"], [(ps[B][:, k:H:16], gj(T.gg, k), T.i32[:, (k + t) % 16:128:16], True, True, 256)
+                                          for k in range(4 * q, 4 * q + 4)])
+        act(H, [B + ".0"], [k_("n32")], af(T.n32[:, c], sl(B, 0), AF.Identity))
+        act(H, [B + ".0"], [k_("nr")], af(T.nr[:, c], sl(B, 0), AF.Identity, 128.0, 1.0 / 4096))
+        mm([k_("n32"), k_("nr"), "i32", "n4k"], [B + ".1"],
+           [(sl(B, 1), T.nr[:, c], T.n4k[:], True, False, 128), (sl(B, 1), T.n32[:, c], T.i32[:], False, True, 512)])
+        dve(H, [B + ".1"], [k_("nu")], ts(T.nu[:, c], sl(B, 1), 128.0 * 4096, None, OP.add))
+        dve(H, [k_("nu")], [k_("n16")], cp(T.n16[:, c], T.nu[:, c]), 0.5)
+        zk = []
+        for e, i0, i1 in GATH_Z[h]:
+            src = T.tab[:, 0:2048].indirect(T.nu[:, H * h + i0:H * h + i1])
+            out = T.zz[:, q0 + 16 * i0:q0 + 16 * i1]
+            zk.append(k_("z%d" % i0))
+            if e == "act":
+                act(16 * (i1 - i0), TAB + [k_("nu")], zk[-1:], af(out, src, AF.Identity, 128.0, 1.0 / 4096), GC)
+            else:
+                dve(16 * (i1 - i0), TAB + [k_("nu")], zk[-1:], ts(out, src, 1.0 / 4096, 128.0, OP.mult, OP.add), GC)
+        mm([k_("fx0"), k_("fx2"), "ib"], [D + ".0"], group(sl(D, 0), [(T.ib[:], kk(T.fx, k)) for k in range(16)]))
+        act(H, [D + ".0"], [k_("bad")], step(T.bad[:, c], sl(D, 0), 8.5))
+        mm([k_("fx0"), k_("fx2"), "zs"], [B + ".3"], group(sl(B, 3), [(T.zs[:, 15 - k:143 - k], kk(T.fx, k)) for k in range(16)]))
+        act(H, [B + ".3"], [k_("a")], step(T.a[:, c], sl(B, 3), 4.5, -1.0))
+        act(H, [B + ".3"], [k_("pc")], af(T.pc[:, c], sl(B, 3), AF.Identity))
+        mm([k_("bad"), "tri"], [D + ".1"], group(sl(D, 1), [(T.tri[:], T.bad[:, c])]))
+        act(H, [D + ".1", "pm"], [k_("m")], step(T.m[:, c], sl(D, 1), PM))
+        mm([k_("a"), "bo"], [D + ".2"], group(sl(D, 2), [(T.bo[:], T.a[:, c])]))
+        act(H, [D + ".2", "thr"], [k_("nl"), k_("acc")],
+            step(T.nl[:, c], sl(D, 2), T.thr[:, 0:1], 1.0, None if last else T.acc[:, 4 * h:4 * h + 1]))
+        mm([k_("a"), k_("nl"), "ibig", C + ".1"], [C + ".1"],
+           group(sl(C, 1), [(T.a[:, c], T.ibig[:]), (T.nl[:, c], T.ibig[:])], False, 128, False))
+        mm([k_("m"), "fw"], slots(A), [(sl(A, j), T.fw[:], T.m[:, c], True, True, 128) for j in range(4)])
+        dve(512, [k_("wp")] + slots(A), [k_("tp")], tt(tq, wq, ps[A][:], OP.mult))
+        mm([k_("tp"), "sj"], [B + ".2"],
+           [(ps[B][:, 2 * H + j:3 * H:4], T.tp[:, 512 * h + H * j:512 * h + H * (j + 1)], T.sj[:], True, True, 256) for j in range(4)])
+        dve(H, [B + ".2"], [k_("ra")], ts(T.ra[:, c], sl(B, 2), CK, -CK - 160.0, OP.add, OP.add))
+        dve(H, [B + ".2", k_("ra")], [k_("dr")], tt(T.dr[:, c], sl(B, 2), T.ra[:, c], OP.subtract))
+        mm([k_("dr"), "ib", C + ".1"], [C + ".1"], group(sl(C, 1), [(T.ib[:], T.dr[:, c])], False))
+        dve(H, [k_("dr")], [k_("fo")], ts(T.fo[:, c], T.dr[:, c], CD - 160.0, CD, OP.add, OP.not_equal), 0.5)
+        dve(H, [C + ".1", "rst"], [k_("mins")],
+            lambda: ve.tensor_tensor_scan(T.mins[:, c], T.rst[:], sl(C, 1), 131072.0, OP.max, OP.min))
+        mb = lambda: T.mins[:, c].indirect(T.ends[:])
+        dve(H, [k_("mins"), "ends"], [k_("rb")], ts(T.rb[:, c], mb(), CK, -CK, OP.add, OP.add), GC)
+        dve(H, [k_("mins"), "ends", k_("rb")], [k_("dbc")], tt(T.dbc[:, c], mb(), T.rb[:, c], OP.subtract), GC)
+        mm([k_("dbc"), "ib"], [D + ".3"], group(sl(D, 3), [(T.dbc[:, c], T.ib[:])]))
+        mm([k_("dbc"), k_("dr"), "ib", "nib"], [C + ".0"], group(sl(C, 0), [(T.ib[:], T.dr[:, c]), (T.nib[:], T.dbc[:, c])]))
+        dve(H, [D + ".3", k_("m")], [D + ".3"], tt(sl(D, 3), T.m[:, c], sl(D, 3), OP.mult))
+        dve(H, [D + ".3", ky], [kyn], tt(YN, Y, sl(D, 3), OP.add))
+        send([kyn], ["yi%d%d" % (t + 1, h)], T.yi[:, o1:o1 + H], YN)
+        dve(H, [C + ".0"], [k_("fn")], ts(T.fn[:, c], sl(C, 0), CD - 160.0, CD, OP.add, OP.not_equal))
+        mm([k_("fn"), k_("fo"), k_("pc"), "ib", "nib"], [C + ".2"],
+           group(sl(C, 2), [(T.ib[:], T.pc[:, c]), (T.fo[:, c], T.nib[:]), (T.fn[:, c], T.ib[:])]))
+        act(H, [C + ".2"], [k_("a2")], step(T.a2[:, c], sl(C, 2), 4.5, -1.0))
+        mm([k_("a2"), "w2"], [D + ".2"], group(sl(D, 2), [(T.w2[:], T.a2[:, c])]))
+        act(H, [D + ".2"], [k_("wa")], step(T.wa[:, c], sl(D, 2), 27.5))
+        mm([k_("wa"), "i16"], [C + ".3", C + ".1"], group(sl(C, 3), [(T.wa[:, c], T.i16[:])], True, 128, False))
+        if h == 1:
+            at = ps[D][:, H:H + 16]
+            mm(["yq%d0" % t, kyn, "zw"], [D + ".1"],
+               group(at, [(T.zw[:, 15 - j:143 - j], T.yq[:, 256 * t + j:256 * t + 256:16]) for j in range(16)], True, 64))
+            dve(16, [D + ".1"], ["ca"], cp(T.ca[:], at))
+            dve(16, ["ca"], ["cb"], ts(T.cb[:], T.ca[:], 7, None, OP.bitwise_and))
+            dve(16, ["cb", "base0"], ["cc"], tt(T.cc[:], T.cb[:], T.base[:], OP.add))
+            dve(16, ["cc"], ["col"], cp(T.col[:], T.cc[:]))
+        for q in range(4):
+            b = (B, A)[q % 2]
+            calls = []
+            for j in range(4):
+                calls += group(sl(b, j), [(T.ib[:], gj(T.zz, 4 * q + j)), (T.nib[:], YN)])
+            mm(zk + [kyn, "ib", "nib"], slots(b), calls)
+            if q in FZ_ACT[h]:
+                act(512, slots(b), [k_("az%d" % q)], af(ch(T.az, q), ps[b][:], AF.Abs, -128.0))
+                dve(512, [k_("az%d" % q)], [k_("fz%d" % q)], ts(ch(T.fz, q), ch(T.az, q), 2.5, None, OP.is_gt), 0.5)
+            else:
+                dve(512, slots(b), [k_("fz%d" % q)], ts(ch(T.fz, q), ps[b][:], CD - 128.0, CD, OP.add, OP.not_equal))
+            mm([k_("fz%d" % q), "g8", C + ".3"], [C + ".3"],
+               [(ps[C][:, 3 * H + k:4 * H:16], kk(T.fz, k), T.g8[:], False, k == 15, 64) for k in range(4 * q, 4 * q + 4)])
+        uw = [(T.wh[:], YN), (T.wl[:], YN)]
+        mm([kyn, "wh", "wl", "ih", "cu"], [D + ".0"], group(sl(D, 0), [(T.ih[:], T.cu[:])] + uw))
+        dve(H, [D + ".0"], [k_("ur")], ts(T.ur[:, c], sl(D, 0), CU, -CU, OP.add, OP.add))
+        mm([kyn, "wh", "wl", "ih", "c32", "nib", k_("ur")], [D + ".1"],
+           group(sl(D, 1), [(T.ih[:], T.c32[:])] + uw + [(T.nib[:], T.ur[:, c])]))
+        dve(H, [D + ".1", k_("r16")], [k_("pp")], tt(T.pp[:, c], T.r16[:, c], sl(D, 1), OP.mult))
+        dve(H, [k_("pp"), "pfar"], [k_("pq")], ts(T.pq[:, c], T.pp[:, c], PF, None, OP.add))
+        dve(H, [k_("pq")], [k_("far")], ts(T.far[:, c], T.pq[:, c], 5, 2047, OP.arith_shift_right, OP.bitwise_and))
+        mm([k_("n16"), "ih"], [D + ".2"], group(sl(D, 2), [(T.ih[:], T.n16[:, c])]))
+        dve(H, [k_("far"), D + ".2"], [k_("fmn")], tt(T.fmn[:, c], T.far[:, c], sl(D, 2), OP.subtract))
+        mm([k_("a2"), "w1"], [D + ".0"], group(sl(D, 0), [(T.w1[:], T.a2[:, c])]))
+        dve(H, [D + ".0"], [k_("m1")], ts(T.m1[:, c], sl(D, 0), CM, CM + 8.0, OP.add, OP.is_equal))
+        mm([k_("n16"), k_("r16"), "ih", "nih"], [D + ".1"], group(sl(D, 1), [(T.ih[:], T.n16[:, c]), (T.nih[:], T.r16[:, c])]))
+        dve(H, [D + ".1", k_("m1")], [k_("t1")], tt(T.t1[:, c], T.m1[:, c], sl(D, 1), OP.mult))
+        act(H, [C + ".3"], [k_("tf")], step(T.tf[:, c], sl(C, 3), 20.5))
+        mm([k_("tf"), "ib"], [D + ".2"], group(sl(D, 2), [(T.tf[:, c], T.ib[:])]))
+        parts = [T.r16[:, c], T.t1[:, c], T.hh[:, c]]
+        pk = [k_("r16"), k_("t1"), k_("hh")]
+        if not last:
+            mm(pk[:2] + ["ih", "i4k", kyn], [D + ".0"], group(sl(D, 0), [(T.i4k[:], YN)] + [(T.ih[:], p) for p in parts[:2]]))
+            act(H, [D + ".0"], [k_("cn")], af(T.cn[:, c], sl(D, 0), AF.Identity))
+            dve(H, [D + ".2", k_("fmn")], [k_("hh")], tt(T.h32[:, c], T.fmn[:, c], sl(D, 2), OP.mult))
+            mm(pk + ["ih", "i32"], [D + ".3"],
+               group(sl(D, 3), [(T.ih[:], p) for p in parts[:2]], True, 128, False) + [(sl(D, 3), T.i32[:], T.h32[:, c], False, True, 512)])
+            dve(H, [D + ".3"], ["uq%d%d" % (t, h)], cp(T.uq[:, o0:o0 + H], sl(D, 3)))
+            send(["uq%d%d" % (t, h)], ["ui%d%d" % (t + 1, h)], T.ui[:, o1:o1 + H], T.uq[:, o0:o0 + H])
+        else:
+            dve(H, [D + ".2", k_("fmn")], [k_("hh")], tt(T.hh[:, c], T.fmn[:, c], sl(D, 2), OP.mult))
+            mm(pk + ["ih"], [D + ".3"], group(sl(D, 3), [(T.ih[:], p) for p in parts]))
+            mm(pk + ["wz"], [B + ".0"], group(sl(B, 0), [(T.wz[:], p) for p in parts]))
+            dve(H, [D + ".3"], [k_("rq")], cp(T.rq[:, c], sl(D, 3)))
+            send([k_("rq")], [k_("ri")], T.ri[:, c], T.rq[:, c])
+            act(H, [B + ".0"], [k_("cn")], af(T.cn[:, c], sl(B, 0), AF.Identity))
+
+    YZ = ["yzt%d" % q for q in range(4)]
+    for t in range(V):
+        visit[0] = t
+        half(t, 0)
+        half(t, 1)
+        for h in (0, 1):
+            c, at = slice(H * h, H * h + H), T.col[:, 8 * h:8 * h + 8]
+            if t < V - 1:
+                dve(H, ["cn_%d" % h, "hh_%d" % h, "col"] + TAB, TAB,
+                    tt(T.tab[:, 0:2048].indirect(at), T.cn[:, c], T.h32[:, c], OP.add), SC)
+            else:
+                dve(H, ["cn_%d" % h, "col"] + YZ, YZ, cp(T.yzt[:, 0:2048].indirect(at), T.cn[:, c]), SC)
+        if t < V - 1:
+            mm(["acc_0", "acc_1", "o16"], ["A1.1"], [(ps["A1"][:, H:H + 1], T.o16[:], T.acc[:, 4 * h:4 * h + 1], h == 0, h == 1, 256)
+                                                     for h in (0, 1)])
+            dve(1, ["A1.1"], ["ai"], cp(T.ai[:, 0:1], ps["A1"][:, H:H + 1]))
+            dve(1, ["ai"], ["aj"], ts(T.aj[:, 0:1], T.ai[:, 0:1], 1, None, OP.bitwise_and))
+            dve(1, ["aj"], ["thr"], ts(T.thr[:, 0:1], T.aj[:, 0:1], -1000.0, -4500.0, OP.mult, OP.add))
+    dma("sp", 2.0, ["yi40", "yi41"], [], T.yo[:], T.yi[:, 1024:1280])
+    dma("sp", 2.0, YZ, [], T.yz[:], T.yzt[0:128:16, :])
+    dma("sp", 2.0, ["ri_0"], [], T.yj[:, 0:H], T.ri[:, 0:H])
+    dma("act", 2.0, ["ri_1"], [], T.yj[:, H:2 * H], T.ri[:, H:2 * H])
+    return ops, nen
+
+
+def order(ops):
+    LAT = COST["lat"]
+    writer, readers = {}, {}
+    for i, o in enumerate(ops):
+        raw = set(writer[k] for k in o["r"] if k in writer)
+        oth = set()
+        for k in o["w"]:
+            if k in writer:
+                oth.add(writer[k])
+            oth.update(readers.get(k, ()))
+        oth.discard(i)
+        o["raw"], o["oth"] = raw, oth - raw
+        for k in o["r"]:
+            readers.setdefault(k, []).append(i)
+        for k in o["w"]:
+            writer[k] = i
+            readers[k] = []
+    n = len(ops)
+    cost = [o["cost"] for o in ops]
+    hold = [o["cost"] if o["kind"] == "c" else 0.1 for o in ops]
+    eng = [o["eng"] for o in ops]
+    pred = [[(p, 0.0 if eng[p] == eng[i] and ops[p]["kind"] == "c" and (p not in o["raw"] or eng[i] == "pe") else LAT)
+             for p in sorted(o["raw"] | o["oth"])] for i, o in enumerate(ops)]
+    back = [[] for _ in ops]
+    for i in range(n):
+        for p, gap in pred[i]:
+            back[p].append((i, gap))
+
+    def place(keys, before, after, turned):
+        left = [len(b) for b in before]
+        ready = [i for i in range(n) if left[i] == 0]
+        start, busy = [0.0] * n, {}
+        while ready:
+            i = min(ready, key=lambda x: keys[x])
+            ready.remove(i)
+            s = max([start[p] + cost[p] + gap for p, gap in before[i]] or [0.0])
+            lead = cost[i] - hold[i] if turned else 0.0
+            moved = True
+            while moved:
+                moved = False
+                for r in [eng[i]] + ops[i]["banks"]:
+                    for a, b, e in reversed(busy.get(r, ())):
+                        pad = 0.0 if e == eng[i] else LAT
+                        if b + pad <= s + lead - 6.0:
+                            break
+                        if a - pad < s + lead + hold[i] - 1e-9 and b + pad > s + lead + 1e-9:
+                            s = b + pad - lead
+                            moved = True
+            start[i] = s
+            for r in [eng[i]] + ops[i]["banks"]:
+                lst = busy.setdefault(r, [])
+                lst.append((s + lead, s + lead + hold[i], eng[i]))
+                j = len(lst) - 1
+                while j > 0 and lst[j - 1][0] > lst[j][0]:
+                    lst[j - 1], lst[j] = lst[j], lst[j - 1]
+                    j -= 1
+            for x, gap in after[i]:
+                left[x] -= 1
+                if left[x] == 0:
+                    ready.append(x)
+        return start, max(start[i] + cost[i] for i in range(n))
+
+    if "start" not in MEMO:
+        tail = [0.0] * n
+        for i in range(n - 1, -1, -1):
+            tail[i] = cost[i] + max([tail[x] + gap for x, gap in back[i]] or [0.0])
+        def by(ranking):
+            keys = [0.0] * n
+            for i in range(n - 1, -1, -1):
+                if ops[i]["cls"] is not None:
+                    keys[i] = 1000.0 * ops[i]["at"] + ranking.get(ops[i]["cls"], 0.0)
+                elif ops[i]["kind"] == "dma" and ops[i]["at"] < 0:
+                    keys[i] = i - 1.0e6
+                else:
+                    keys[i] = min([keys[x] for x, gap in back[i]] or [1.0e6]) - cost[i]
+            return place(keys, pred, back, False)
+        MEMO["by"], MEMO["tail"] = by, tail
+        MEMO["start"] = by({k: float(j) for j, k in enumerate(RANKING.split())}) if RANKING else \
+            place([-v for v in tail], pred, back, False)
+    start, end = MEMO["start"]
+    seq = sorted(range(n), key=lambda i: (start[i], i))
+    bank = {}
+    for i in seq:
+        o = ops[i]
+        o["start"] = start[i]
+        o["bk"] = set(bank[b][e] for b in o["banks"] for e in bank.get(b, {}) if e != eng[i])
+        for b in o["banks"]:
+            bank.setdefault(b, {})[eng[i]] = i
+    return seq, end
+
+
+def rank_program(g, core, T, topo):
+    if T.rank_of(core) is None:
+        return
+    ops, nen = plan(g, core, T, topo)
+    seq = order(ops)[0]
+    queue = {"pe": g.tensor, "act": g.scalar, "dve": g.vector, "pool": g, "sp": g.sync}
+    count = {"pe": 0, "act": 0, "dve": 0, "pool": 0}
+    mark, seen, top = {}, {e: {} for e in queue}, {}
+    ndma = nsend = 0
+    for i in seq:
+        o = ops[i]
+        e = o["eng"]
+        need = {}
+        for p in o["raw"] | o["oth"] | o["bk"]:
+            po = ops[p]
+            if po["kind"] == "c" and po["eng"] == e and (p not in o["raw"] or e == "pe"):
+                continue
+            s, v = mark[p]
+            need[s] = max(need.get(s, 0), v)
+        for s in sorted(need):
+            if seen[e].get(s, 0) < need[s]:
+                queue[e].wait_ge(T.sem[s], need[s])
+                seen[e][s] = need[s]
+        if o["kind"] == "c":
+            count[e] += 1
+            mark[i] = ("c" + e, count[e])
+            o["emit"]().then_inc(T.sem["c" + e], 1)
+        elif o["kind"] == "dma":
+            mark[i] = ("dm%d" % ndma, 16)
+            ndma += 1
+            o["emit"]().then_inc(T.sem[mark[i][0]], 16)
+        else:
+            mark[i] = ("ar%d" % nsend, nen)
+            nsend += 1
+            o["emit"](T.sem[mark[i][0]])
+        top[mark[i][0]] = mark[i][1]
+    top["sent"] = nsend * nen
+    for s in sorted(top):
+        g.wait_ge(T.sem[s], top[s])

@@ -1,3 +1,4 @@
+import numpy as np
 from concourse.mybir import AluOpType as OP, ActivationFunctionType as AF
 
 V = 4
@@ -15,67 +16,46 @@ SCRATCH = {
     "yi": _sb(256 * 5, BF), "ui": _sb(256 * 4, U16), "yq": _sb(256 * 4, BF), "uq": _sb(256 * 3, U16),
     "rq": _sb(256, F32), "ri": _sb(256, F32),
     "gg": _sb(4096, F32), "zz": _sb(4096, BF), "d": _sb(4096, BF), "fx": _sb(4096, BF), "ad": _sb(4096, BF),
-    "fz": _sb(4096, BF), "az": _sb(4096, BF), "wp": _sb(1024, F32), "tp": _sb(1024, F32),
-    "dif": _sb(128, F32), "gm": _sb(128, F32), "gj": _sb(128, F32), "g4": _sb(32, F32), "zc": _sb(144, F32),
+    "fz": _sb(4096, BF), "dz": _sb(4096, BF), "tp": _sb(1024, F32),
+    "dif": _sb(128, F32), "gm": _sb(128, F32), "g4": _sb(32, F32), "zc": _sb(144, F32),
     "pi": _sb(8, I32), "pj": _sb(8, I32), "pf": _sb(32, F32),
-    "i32": _sb(128, F32), "ib": _sb(128, BF), "ih": _sb(128, F16), "nih": _sb(128, F16), "nib": _sb(128, BF), "bo": _sb(128, BF),
-    "i4k": _sb(128, BF), "n4k": _sb(128, BF), "ibig": _sb(128, BF), "i16": _sb(128, BF), "tri": _sb(128, BF), "tmp": _sb(128, BF),
-    "w1": _sb(128, BF), "w2": _sb(128, BF), "zs": _sb(144, BF), "zw": _sb(144, BF), "g8s": _sb(8, BF),
-    "g8": _sb(8, BF), "wh": _sb(128, BF), "wl": _sb(128, BF), "wz": _sb(128, F16), "wz32": _sb(128, F32), "wz4": _sb(128, BF),
-    "nwz4": _sb(128, BF), "c128": _sb(512, BF), "c160": _sb(128, BF), "cu": _sb(128, F16), "c32": _sb(128, F16),
-    "pk": _sb(144, BF), "fw": _sb(128, BF), "sj": _sb(32, F32),
+    "i32": _sb(128, F32), "ib": _sb(128, BF), "ih": _sb(128, F16), "n2h": _sb(128, F16), "nib": _sb(128, BF), "bo": _sb(128, BF),
+    "i4k": _sb(128, BF), "n4k": _sb(128, BF), "n2k": _sb(128, BF), "ibig": _sb(128, BF), "i16": _sb(128, BF),
+    "tri": _sb(128, BF), "ntri": _sb(128, BF), "tmp": _sb(128, BF), "dig": _sb(512, BF), "wf": _sb(2048, BF),
+    "w1": _sb(128, BF), "w2": _sb(128, BF), "zs": _sb(144, BF), "zt": _sb(144, BF), "zw": _sb(144, BF),
+    "g8s": _sb(8, BF), "g8": _sb(8, BF), "wh": _sb(128, BF), "wl": _sb(128, BF), "wz": _sb(128, F16), "wz32": _sb(128, F32),
+    "wz4": _sb(128, BF), "nwz": _sb(128, BF), "c160": _sb(512, BF), "cu": _sb(128, BF), "wu": _sb(128, BF), "cw": _sb(128, BF),
+    "sj": _sb(32, F32),
     "ini": _sb(128, BF), "rst": _sb(128, F32), "o16": _sb(128, F32), "ends": _sb(8, U16), "endi": _sb(8, I32),
     "base": _sb(16, I32), "wcol": _sb(16, F32), "wcb": _sb(16, BF),
     "r16": _sb(256, F16), "n32": _sb(256, F32), "nr": _sb(256, BF), "nu": _sb(256, U16), "n16": _sb(256, F16),
     "a": _sb(256, BF), "pc": _sb(256, BF), "nl": _sb(256, BF), "bad": _sb(256, BF), "m": _sb(256, BF), "fo": _sb(256, BF), "fn": _sb(256, BF),
-    "ra": _sb(256, F32), "dr": _sb(256, BF), "mins": _sb(256, F32), "rb": _sb(256, F32), "dbc": _sb(256, BF), "a2": _sb(256, BF),
-    "m1": _sb(256, F16), "wa": _sb(256, BF), "tf": _sb(256, BF), "ur": _sb(256, BF), "pp": _sb(256, F32), "pq": _sb(256, I32),
-    "far": _sb(256, I32), "fmn": _sb(256, F16), "t1": _sb(256, F16), "hh": _sb(256, F16), "h32": _sb(256, F32),
-    "cn": _sb(256, F32), "ca": _sb(16, I32), "cb": _sb(16, I32), "cc": _sb(16, I32), "col": _sb(16, U16),
+    "ra": _sb(256, F32), "dr": _sb(256, BF), "mins": _sb(256, F32), "rb": _sb(16, F32), "db": _sb(32, BF), "dbc": _sb(256, BF),
+    "a2": _sb(256, BF), "m1": _sb(256, BF), "wa": _sb(256, BF), "tf": _sb(256, BF), "ur": _sb(256, F16), "pp": _sb(256, F32),
+    "pq": _sb(256, I32), "far": _sb(256, I32), "t1": _sb(256, F16), "t2": _sb(256, F32), "t2h": _sb(256, F16),
+    "cn": _sb(256, F32), "w16": _sb(256, F16), "sy": _sb(256, F32),
+    "ca": _sb(16, I32), "cb": _sb(16, I32), "cc": _sb(16, I32), "col": _sb(16, U16),
     "acc": _sb(8, F32), "ai": _sb(8, I32), "aj": _sb(8, I32), "thr": _sb(8, F32),
 }
-for _b in ("A0", "A1", "B0", "B1", "C0", "C1", "D0", "D1"):
+BANKS = ("A0", "A1", "B0", "B1", "C0", "C1", "D0", "D1")
+for _b in BANKS:
     SCRATCH["ps" + _b] = ("psum", [128, 512], F32)
 
 SEMAPHORES = (["cpe", "cact", "cdve", "cpool", "sent"] + ["dm%d" % i for i in range(16)]
               + ["ar%d" % i for i in range(16)])
 
-GATH_G = [[("act", 0, 64), ("dve", 64, 128)], [("act", 0, 64), ("act", 64, 128)]]
-GATH_Z = [[("act", 0, 32), ("act", 32, 64), ("act", 64, 96), ("act", 96, 128)]] * 2
-HX_ENG = ["dve", "act", "dve", "act"]
-FZ_ACT = [(), ()]
-COST = {"cyc": 0.00100, "pec": 0.00050, "ovh": 0.06, "pov": 0.005, "lat": 0.12, "gc": 1.55, "sc": 3.8, "net": 2.5}
+CFG = {
+    "gx": [[("act", 0, 64), ("dve", 64, 128)], [("act", 0, 64), ("act", 64, 128)]],
+    "gz": [[("act", 0, 64), ("act", 64, 128)]] * 2,
+    "zs": [["dve", "pe", "pe", "pe"], ["dve", "pe", "pe", "pe"]],
+    "nom": 1, "yz": "inc", "hx": ["dve", "act", "dve", "act"],
+    "at": {"y": "D3", "nom": "B0", "nt": "B1", "v": "D0", "tri": "D1", "c": "D2", "key": "C1", "dr": "B2", "dl": "D3",
+           "dn": "C0", "a2": "C2", "w2": "D2", "tf": "C3", "col": "D1", "u": "D0", "w1": "D1", "p1": "D1", "p2": "D2",
+           "cn": "D0", "uq": "D3", "yz": "B0", "yn": "D3"},
+    "passes": 1500, "seed": 1, "shake": 2.0, "span": 6.0, "slack": 0.05,
+}
+COST = {"cyc": 0.00083, "pec": 0.000417, "lat": 0.12, "gc": 1.55, "sc": 3.8, "net": 2.4, "ind": 0.055}
 MEMO = {}
-RANKING = """
-awa_1a dd0_0a pC00c awa_0a pC00b dd0_1a ddbc_1a anr_1a dd2_0a pui0a ayzt0a pB00c dfz1_0a ag0_0a az0_0a pA00a drq_0a
-dmins_0a ag0_1a pB00a az64_0a dd1_0a anr_0a dg64_0a am_0a dfz0_1a dfx2_0a az0_1a pB10a dfx2_1a pD00a pD03a dyq1a pC11d
-pA10g dd1_1a ddr_0a dd3_0a dra_0a anl_1a dhh_1a dn16_1a dfn_1a ag64_1a aad0_1a dcaa dfx0_0a dmins_1a pD10a awp_0a dm1_0a
-pA00d pD01a pC11a aad2_0a dd2_1a dfx0_1a daja an32_0a aad0_0a pC02a pD03b dd3_1a pD13a pA00c pA00b abad_1a dr16_0a
-anl_0a dt1_1a dn16_0a pB00b aa2_1a aad2_1a pC10b pA10c pD11c pB10e az32_0a pA10a ahx1a pC00a dpq_1a pA00e pC10a drb_0a
-abad_0a pA10b aa2_0a pyzp3a ahx3a ddr_1a pC01d dtp_1a pB00d pB10b drq_1a pA00g an32_1a pC01a pD02a pD12a pA10d pC10c
-dr16_1a dtp_0a aa_0a pD11a pC13a pB01a pA00f pD12b dfz2_1a awp_1a az32_1a az96_1a pyi0a pB10c pC03e az96_0a pA10e drb_1a
-pyzp1a pD12c pC11c am_1a pC01c pD00c pC01b pC11b ddbc_0a dnu_0a pB00f pC12a pC00d pyzp2a aa_1a pB11a dra_1a ayzt3a dD03a
-dpq_0a pB00e dfn_0a dthra pD02b pC03d dfz3_0a dfz0_0a pB10d pyi1a dfz2_0a pD01b pD13b dpp_1a ahx2a dD13a dtab0a dfar_1a
-dhh_0a dfo_0a pD01c dpp_0a pD10b pB12a dnu_1a dyq0a pD03d pD03c pyzp0a pD10c dfz1_1a pC03a pD13c duq0a acn_0a pB00g
-dyzt0a dcca pD00b dm1_1a dur_1a pA00h pC13d dcba pA10h pD11b pC03b pD13d daia ahx0a pC13b pD02c ayzt2a dfo_1a pB10f
-dur_0a az64_1a pC13e dtab0b ayzt1a pA10f atf_1a pA11a dfmn_1a pC13c pC10d dfar_0a atf_0a pri_0a acn_1a dt1_0a pui1a
-pC03c dyzt0b dfz3_1a dfmn_0a pB10g duq1a dcola pri_1a
-"""
-RANKING = """
-dra_1a ag0_0a dg64_0a pyzp1a pD03a dfx0_1a pD13a dhx0a pyzp0a aa_0a dd0_0a dd1_0a dd2_0a dd3_0a ahx1a ag0_1a ag64_1a
-dfx0_0a dfx2_0a dhx2a ayzt0a ayzt3a pA00b pyzp2a pD00a pB00a pA00c dd0_1a dd1_1a dd2_1a dd3_1a pD01a ahx3a pA00d aad0_0a
-pB00b aad2_0a pA10a pB03a awp_0a abad_0a pC00a pB00d ayzt2a pB00c dfx2_1a am_0a pD10a pA10b pC01a pC10a ayzt1a pD00b
-pA00a pB10a pA10c pyzp3a pC01b dtp_0a an32_0a pA00e pD02a dr16_0a pA10d anr_0a pB10b aad2_1a pB01a pB13a awp_1a pB02a
-pC01c abad_1a aad0_1a anl_0a pB12a pB10c pD11a az32_0a am_1a dra_0a az0_0a az64_0a az96_0a pA10e pB10d aa_1a dnu_0a
-pC11b pC01d dtp_1a pD12a dr16_1a ddr_0a an32_1a anr_1a anl_1a pui0a drb_0a apc_0a pC11c dfz0_0a pB11a ddbc_0a dnu_1a
-dn16_0a dD03a az0_1a az32_1a az64_1a ddr_1a dyq0a pC11d pC00b pB00e pA00f dfn_0a pC02a drb_1a pC11a dpq_0a dmins_1a
-dmins_0a pD03b ddbc_1a dfz1_0a aa2_0a pD13b dur_0a pC13e dn16_1a dD13a pD01b awa_0a dfo_1a pB00f apc_1a pC03a dyq1a
-dpp_0a pC10b az96_1a pC03b pD00c pD02c pB10e pA00g pA10f dfz2_0a dfn_1a pC03c dfz3_0a pD12d dfo_0a dfar_0a dm1_0a pC12a
-pD01c pD11b pD10b dfmn_0a dfz0_1a dt1_0a pC03d dfz1_1a pC03e pD12b dur_1a aa2_1a pyi0a atf_0a dcaa pB10f pD11c pA10g
-dfz3_1a dfz2_1a pD02d pC13a pyi1a pD00d dhh_0a dpp_1a pC13b pD10c pD12c acn_0a pD03c dm1_1a dpq_1a pC13c dfar_1a drq_0a
-pD11d duq0a pC13d dfmn_1a pB00g dt1_1a awa_1a pD02b dcba atf_1a duq1a dcca pri_0a dhh_1a pD13c pri_1a pD10d drq_1a
-acn_1a pui1a dtab0a dyzt0a dtab0b dyzt0b pA11a daia dcola dthra daja pB10g
-""".strip()
 
 
 def plan(g, core, T, topo):
@@ -85,26 +65,21 @@ def plan(g, core, T, topo):
     mask = topo.mask(core, nxt)
     nen = len(topo.engines(core, nxt))
     ve, ac, pe = g.vector, g.scalar, g.tensor
-    CYC, PEC, OVH, POV, GC, SC, NET = [COST[k] for k in ("cyc", "pec", "ovh", "pov", "gc", "sc", "net")]
-    ops, visit, seen = [], [-1], {}
+    CYC, PEC, GC, SC, NET, IND = [COST[k] for k in ("cyc", "pec", "gc", "sc", "net", "ind")]
+    ops = []
 
     def op(eng, cost, reads, writes, emit, kind="c"):
         banks = sorted(set(k[:2] for k in list(reads) + list(writes) if len(k) == 4 and k[2] == "."))
-        cls = None
-        if visit[0] >= 0 and kind != "dma":
-            name = writes[0].replace(".", "")
-            if name[:2] in ("yi", "ui", "yq", "uq") and name[2:].isdigit():
-                name = name[:2] + name[3:]
-            seen[(visit[0], eng, name)] = seen.get((visit[0], eng, name), -1) + 1
-            cls = "%s%s%s" % (eng[0], name, "abcdefghijkl"[seen[(visit[0], eng, name)]])
-        ops.append({"eng": eng, "cost": cost, "r": list(reads), "w": list(writes), "emit": emit, "kind": kind, "banks": banks,
-                    "cls": cls, "at": visit[0]})
+        ops.append({"eng": eng, "cost": cost, "r": list(reads), "w": list(writes), "emit": emit, "kind": kind, "banks": banks})
+
+    def price(n_el, f):
+        return (IND if f in (GC, SC) else 0.0) + max(64, n_el * f) * CYC
 
     def dve(n_el, reads, writes, emit, f=1.0, calls=1):
-        op("dve", calls * (OVH + max(64, n_el * f) * CYC), reads, writes, emit)
+        op("dve", calls * price(n_el, f), reads, writes, emit)
 
     def act(n_el, reads, writes, emit, f=1.0):
-        op("act", OVH + max(64, n_el * f) * CYC, reads, writes, emit)
+        op("act", price(n_el, f), reads, writes, emit)
 
     def many(emits):
         def emit():
@@ -114,8 +89,14 @@ def plan(g, core, T, topo):
             return last
         return emit
 
-    def mm(reads, writes, calls):
-        op("pe", 0.03 + sum(c[5] * PEC + POV for c in calls), reads, writes,
+    def mm(reads, writes, calls, more=False):
+        reads, writes = list(reads), list(writes)
+        for b in sorted(set(k[:2] for k in writes if len(k) == 4 and k[2] == ".")):
+            if calls[0][3] and calls[-1][4] and not more:
+                reads.append(b + ".o")
+            else:
+                writes.append(b + ".o")
+        op("pe", sum(c[5] * PEC for c in calls), reads, writes,
            many([(lambda c=c: pe.matmul(c[0], c[1], c[2], c[3], c[4])) for c in calls]))
 
     def group(out, terms, start=True, cyc=128, stop=True):
@@ -154,7 +135,7 @@ def plan(g, core, T, topo):
     def slots(b):
         return ["%s.%d" % (b, s) for s in range(4)]
 
-    ps = {b: T["ps" + b] for b in ("A0", "A1", "B0", "B1", "C0", "C1", "D0", "D1")}
+    ps = {b: T["ps" + b] for b in BANKS}
     TAB = ["tab%d" % c for c in range(4)]
 
     dma("sp", 2.2, [], ["lin0"], T.lin[:, 0:512], T.lsr[:, 0:512])
@@ -181,72 +162,76 @@ def plan(g, core, T, topo):
     ramp("gm", T.gm[:], [[1, 8], [0, 16]], 0, 0)
     ramp("zc", T.zc[:], [[1, 144]], -15, 0)
     ramp("ini1", T.ini[:], [[0, 8], [32, 16]], -160, 0)
-    ramp("gj", T.gj[:], [[16, 8], [0, 4], [1, 4]], 0, 0)
-    ramp("g4", T.g4[:], [[1, 32]], 0, 0)
-    ramp("endi", T.endi[:], [[16, 8]], 15, 0, True)
-    ramp("base0", T.base[:], [[128, 16]], 0, 0, True)
-    for key, v in (("i4k", 4096.0), ("ib", 1.0), ("ih", 1.0), ("nih", -1.0)):
+    ramp("g4", T.g4[:], [[1, 8], [0, 4]], 0, 0)
+    ramp("endi", T.endi[:], [[1, 8]], 0, 0, True)
+    ramp("base0", T.base[:], [[0, 2], [128, 8]], 0, 0, True)
+    for key, v in (("i4k", 4096.0), ("ib", 1.0), ("ih", 1.0), ("n2h", -2048.0)):
         dve(128, ["dif"], [key], ts(T[key][:], T.dif[:], 0.0, v, OP.is_equal, OP.mult))
-    for key, v in (("nib", -1.0), ("i32", 1.0), ("n4k", -4096.0), ("ibig", 262144.0), ("i16", 16.0), ("w1", -7.0)):
+    for key, v in (("nib", -1.0), ("i32", 1.0), ("n4k", -4096.0), ("n2k", -2048.0), ("ibig", 262144.0), ("i16", 16.0), ("w1", -7.0)):
         act(128, ["ib"], [key], af(T[key][:], T.ib[:], AF.Identity, 0.0, v))
+    for j in range(4):
+        act(128, ["ib"], ["dig%d" % j], af(T.dig[:, H * j:H * j + H], T.ib[:], AF.Identity, 0.0, 32.0 ** j / 4096))
 
     def lin(key, reads, out, in_, scale, bias=0.0, n_el=1):
         act(n_el, reads, [key], af(out, in_, AF.Identity, bias, scale))
     pint = lambda c: T.pj[:, c:c + 1]
     dve(1, ["pi"], ["pj0"], ts(pint(0), T.pi[:, 0:1], 4, None, OP.arith_shift_right))
     dve(1, ["pi"], ["pj1"], ts(pint(1), T.pi[:, 0:1], 15, None, OP.bitwise_and))
-    dve(1, ["pi"], ["pj2"], ts(pint(2), T.pi[:, 0:1], 2, None, OP.arith_shift_right))
-    dve(1, ["pi"], ["pj3"], ts(pint(3), T.pi[:, 0:1], 2, 3, OP.arith_shift_right, OP.bitwise_and))
-    dve(1, ["pi"], ["pj4"], ts(pint(4), T.pi[:, 0:1], 1, None, OP.bitwise_and))
-    dve(1, ["pi"], ["pj5"], ts(pint(5), T.pi[:, 0:1], 1, 1, OP.arith_shift_right, OP.bitwise_and))
-    PG, PK, P4, PJ, B0, B1, PG16, PM, PF, PZ, P8, PW, PV, PT, PGJ, PGJ3, PW4 = [T.pf[:, c:c + 1] for c in range(17)]
-    dve(6, ["pj%d" % j for j in range(6)], ["pf"], cp(T.pf[:, 0:6], T.pj[:, 0:6]))
+    PG, PK, PG16, PM, PF, PZ, P8, PW, PZ4, PU, PV = [T.pf[:, c:c + 1] for c in range(11)]
+    dve(2, ["pj0", "pj1"], ["pf"], cp(T.pf[:, 0:2], T.pj[:, 0:2]))
     lin("pg16", ["pf"], PG16, PG, 16.0)
     dve(1, ["pf"], ["pm0"], ts(PW, PK, 0.0, None, OP.is_equal))
     lin("pm", ["pm0"], PM, PW, 1000.0, -500.0)
     lin("pfar", ["pf"], PF, PK, 37.0 * 32.0)
     lin("pz", ["pf"], PZ, PK, 1.0, 1.0)
     lin("p8", ["pf"], P8, PK, 8.0)
-    X0, X1, X2, X3, X4 = [T.pf[:, c:c + 1] for c in range(17, 22)]
-    lin("x0", ["pf"], X0, B0, 31.0 / 4096, 1.0 / 4096)
-    lin("x1", ["pf"], X1, B1, 1023.0, 1.0)
-    lin("pw4", ["x0", "x1"], PW4, X0, X1)
-    lin("x2", ["pf"], X2, B0, -31.0 / 32, 1.0)
-    lin("x3", ["pf"], X3, B1, -1023.0 / 1024, 1.0)
-    lin("pv", ["x2", "x3"], PV, X2, X3)
-    lin("pgj", ["pf"], PGJ, PG, 16.0, PJ)
-    lin("pgj3", ["pgj"], PGJ3, PGJ, 1.0, -3.0)
-    lin("pz4", ["pf"], PT, PK, 4096.0, 4096.0)
-    lin("npz4", ["pf"], X4, PK, -4096.0, -4096.0)
-    dve(144, ["zc", "pgj3", "pw4"], ["pk"], ts(T.pk[:], T.zc[:], PGJ3, PW4, OP.is_equal, OP.mult))
-    dve(128, ["gj", "pgj", "pv"], ["fw"], ts(T.fw[:], T.gj[:], PGJ, PV, OP.is_equal, OP.mult))
-    dve(32, ["g4", "pf"], ["sj"], ts(T.sj[:], T.g4[:], P4, None, OP.is_equal))
+    lin("pz4", ["pf"], PZ4, PK, -4096.0, -4096.0)
+    for j in range(4):
+        dve(8, ["g4", "pf"], ["sj%d" % j], ts(T.sj[:, j:32:4], T.g4[:, j:32:4], PG, 32.0 ** -j, OP.is_equal, OP.mult))
+    SJ = ["sj%d" % j for j in range(4)]
     dve(16, ["base0", "p8"], ["base0"], ts(T.base[:], T.base[:], P8, None, OP.add))
     dve(128, ["gm", "pf"], ["bo"], ts(T.bo[:], T.gm[:], PG, None, OP.is_equal))
     dve(144, ["zc", "pg16"], ["zs"], ts(T.zs[:], T.zc[:], PG16, None, OP.is_equal))
+    lin("zt", ["zs"], T.zt[:], T.zs[:], 32.0, 0.0, 144)
     lin("g8", ["bo"], T.g8[:], T.bo[:, 0:128:16], 1.0)
     lin("g8s", ["bo"], T.g8s[:], T.bo[:, 0:128:16], 512.0)
     dve(128, ["dif"], ["tmp"], ts(T.tmp[:], T.dif[:], 0.0, None, OP.is_gt))
-    dve(128, ["tmp", "bo"], ["tmp"], tt(T.tmp[:], T.tmp[:], T.bo[:], OP.mult))
-    dve(128, ["tmp", "ib"], ["tri"], tt(T.tri[:], T.ib[:], T.tmp[:], OP.subtract))
+    dve(128, ["tmp", "bo"], ["tmp"], tt(T.tmp[:], T.tmp[:], T.bo[:], OP.mult), 2.0)
+    dve(128, ["tmp", "ib"], ["tri"], tt(T.tri[:], T.ib[:], T.tmp[:], OP.subtract), 2.0)
     dve(8, ["ib", "tri"], ["tmp"], ts(T.tmp[:, 0:8], T.ib[:, 0:128:16], 17.0, None, OP.mult))
     dve(8, ["tmp", "g8"], ["tri"], tt(T.tri[:, 0:128:16], T.tmp[:, 0:8], T.g8[:], OP.subtract))
-    dve(128, ["w1", "bo"], ["w1"], tt(T.w1[:], T.w1[:], T.bo[:], OP.add))
-    dve(128, ["i16", "bo"], ["w2"], tt(T.w2[:], T.i16[:], T.bo[:], OP.add))
-    dve(128, ["gm", "pf", "pz"], ["wz"], ts(T.wz[:], T.gm[:], PG, PZ, OP.is_equal, OP.mult))
+    lin("ntri", ["tri"], T.ntri[:], T.tri[:], -1.0, 0.0, 128)
+    dve(128, ["w1", "bo"], ["w1"], tt(T.w1[:], T.w1[:], T.bo[:], OP.add), 2.0)
+    dve(128, ["i16", "bo"], ["w2"], tt(T.w2[:], T.i16[:], T.bo[:], OP.add), 2.0)
     lin("wz32", ["bo", "pz"], T.wz32[:], T.bo[:], PZ, 0.0, 128)
-    lin("wz4", ["bo", "pz4"], T.wz4[:], T.bo[:], PT, 0.0, 128)
-    lin("nwz4", ["bo", "npz4"], T.nwz4[:], T.bo[:], X4, 0.0, 128)
+    lin("wz4", ["bo", "pz4"], T.wz4[:], T.bo[:], PZ4, 0.0, 128)
+    if CFG["yz"] == "inc":
+        dve(128, ["wz32"], ["wz"], cp(T.wz[:], T.wz32[:]))
+    else:
+        lin("nwz", ["wz32"], T.nwz[:], T.wz32[:], -1.0, 0.0, 128)
     dve(8, ["endi"], ["ends"], cp(T.ends[:], T.endi[:]))
+    for c, b in enumerate(("C0", "C1", "D0", "D1")):
+        calls = []
+        for j in range(4):
+            k = 4 * c + j
+            calls += group(ps[b][:, H * j:H * j + H], [(T.ib[:], T.zt[:, 15 - k:143 - k]), (T.ib[:], T.ib[:])])
+        mm(["ib", "zt"], slots(b), calls)
+        act(512, slots(b), ["wf%d" % c], af(T.wf[:, 512 * c:512 * c + 512], ps[b][:], AF.Identity))
+    WFK = ["wf%d" % c for c in range(4)]
 
-    def fill(key, ap, v, n_el):
-        dve(n_el, [], [key], lambda: ve.memset(ap, v), 0.5)
-    fill("c160", T.c160[:], -160.0, 128)
-    fill("c128", T.c128[:], 128.0, 512)
-    fill("cu", T.cu[:], -1023.5, 128)
-    fill("c32", T.c32[:], 32.0, 128)
+    def fill(key, ap, v, n_el, after=()):
+        dve(n_el, list(after), [key], lambda: ve.memset(ap, v), 0.5)
+    fill("c160", T.c160[:], 160.0, 512)
+    fill("cw", T.cw[:], -5.15625, 128)
+    for k in range(8):
+        fill("cw", T.cw[:, k:128:16], -5.0 * (k // 4), 8, ["cw"])
+    fill("cu", T.cu[:], 1.0, 128)
+    dve(1, ["pf"], ["pu"], ts(PU, PK, 0.0, 2048.0 * 1024, OP.is_equal, OP.mult))
+    dve(1, ["pf"], ["pv"], ts(PV, PK, 1.0, 2080.0, OP.is_equal, OP.mult))
+    dve(1, ["pu", "pv"], ["pu"], tt(PU, PU, PV, OP.add))
+    lin("wu", ["bo", "pu"], T.wu[:], T.bo[:], PU, 0.0, 128)
     fill("rst", T.rst[:], -1.0e6, 256)
-    dve(8, ["rst"], ["rst"], lambda: ve.memset(T.rst[:, 0:128:16], 131072.0))
+    fill("rst", T.rst[:, 0:128:16], 131072.0, 8, ["rst"])
     fill("o16", T.o16[:], 0.0625, 256)
     fill("thr", T.thr[:, 0:1], -4500.0, 1)
     WF, WLO, W7 = T.wcol[:, 0:1], T.wcol[:, 1:2], T.wcol[:, 2:3]
@@ -261,29 +246,42 @@ def plan(g, core, T, topo):
     dve(256, ["jin"], ["ui00", "ui01"], cp(T.ui[:, 0:256], T.jin[:]))
     for c, b in enumerate(("A0", "A1", "B0", "B1")):
         s = slice(512 * c, 512 * c + 512)
-        mm(["i4k", "xin%d" % (c // 2)], slots(b), [(ps[b][:], T.i4k[:], T.xin[:, s], True, True, 512)])
+        mm(["i4k", "xin%d" % (c // 2)], slots(b), group(ps[b][:], [(T.i4k[:], T.xin[:, s])], True, 512))
         dve(512, slots(b) + ["lin%d" % c], ["tab%d" % c], tt(T.tab[:, s], T.lin[:, s], ps[b][:], OP.add))
+    if CFG["yz"] == "inc":
+        for c, b in enumerate(("C0", "D0", "C1", "D1")):
+            s = slice(512 * c, 512 * c + 512)
+            mm(["tab%d" % c, "xin%d" % (c // 2), "wz4", "wz32"], slots(b),
+               [(ps[b][:], T.wz4[:], T.xin[:, s], True, False, 512), (ps[b][:], T.wz32[:], T.tab[:, s], False, True, 2048)])
+            act(512, slots(b), ["yzt%d" % c], af(T.yzt[:, s], ps[b][:], AF.Identity))
 
-    CX, CD, CM, CU, CK = 1.5 * 2 ** 37, 1.5 * 2 ** 25, 1.5 * 2 ** 26, 1.5 * 2 ** 34, 1.5 * 2 ** 28
+    CX, CD, CM, CK = 1.5 * 2 ** 37, 1.5 * 2 ** 25, 1.5 * 2 ** 26, 1.5 * 2 ** 28
 
     def half(t, h):
         last = t == V - 1
         k_ = lambda s: "%s_%d" % (s, h)
         c = slice(H * h, H * h + H)
-        A, B, C, D = "A%d" % h, "B%d" % h, "C%d" % h, "D%d" % h
+        A, B = "A%d" % h, "B%d" % h
         sl = lambda b, s: ps[b][:, H * s:H * s + H]
+
+        def at(name):
+            p = CFG["at"][name]
+            b = p[0] + (p[2] if len(p) > 2 else "%d" % h)
+            return b, H * int(p[1]), "%s.%s" % (b, p[1])
+        pa = lambda name: ps[at(name)[0]][:, at(name)[1]:at(name)[1] + H]
+        pk = lambda name: at(name)[2]
+        byk = lambda name, k, s: ps[at(name)[0]][:, at(name)[1] + k:at(name)[1] + H:s]
         o0 = 256 * t + H * h
         o1 = o0 + 256
         Y, U, YN = T.yi[:, o0:o0 + H], T.ui[:, o0:o0 + H], T.yq[:, o0:o0 + H]
         ky, ku, kyn = "yi%d%d" % (t, h), "ui%d%d" % (t, h), "yq%d%d" % (t, h)
         q0 = 2048 * h
         ch = lambda buf, q, w=1: buf[:, q0 + 512 * q:q0 + 512 * (q + w)]
-        kk = lambda buf, k: buf[:, q0 + H * k:q0 + H * (k + 1)]
+        kk = lambda buf, s: buf[:, q0 + H * s:q0 + H * (s + 1)]
         gj = lambda buf, k: buf[:, q0 + k:q0 + 2048:16]
-        wq = T.wp[:, 512 * h:512 * h + 512]
-        tq = T.tp[:, 512 * h:512 * h + 512]
+        jur = lambda s: s // 4 + 4 * (s % 4)
         gk = []
-        for e, i0, i1 in GATH_G[h]:
+        for e, i0, i1 in CFG["gx"][h]:
             src = T.tab[:, 0:2048].indirect(T.ui[:, o0 + i0:o0 + i1])
             out = T.gg[:, q0 + 16 * i0:q0 + 16 * i1]
             gk.append(k_("g%d" % i0))
@@ -291,154 +289,189 @@ def plan(g, core, T, topo):
                 act(16 * (i1 - i0), TAB + [ku], gk[-1:], af(out, src, AF.Identity), GC)
             else:
                 dve(16 * (i1 - i0), TAB + [ku], gk[-1:], cp(out, src), GC)
-        mm(["i4k", "c160", ky], [D + ".3"], group(sl(D, 3), [(T.i4k[:], T.c160[:, 0:H]), (T.i4k[:], Y)]))
-        if last:
-            for q in (2 * h, 2 * h + 1):
-                s = slice(512 * q, 512 * q + 512)
-                if HX_ENG[q] == "act":
-                    act(512, TAB, ["hx%d" % q], af(T.hx[:, s], T.tab[:, s], AF.Identity, 128.0, 1.0 / 4096))
-                else:
-                    dve(512, TAB, ["hx%d" % q], ts(T.hx[:, s], T.tab[:, s], 1.0 / 4096, 128.0, OP.mult, OP.add))
-                mm(TAB + ["hx%d" % q, "wz4", "nwz4", "wz32", "c128"], ["yzp%d" % q] + slots(C),
-                   [(ps[C][:], T.wz4[:], T.c128[:], True, False, 512), (ps[C][:], T.nwz4[:], T.hx[:, s], False, False, 512),
-                    (ps[C][:], T.wz32[:], T.tab[:, s], False, True, 2048)])
-                act(512, slots(C), ["yzt%d" % q], af(T.yzt[:, s], ps[C][:], AF.Identity))
-        mm(["ib", "ini1"], slots(C), [(sl(C, 1), T.ib[:], T.ini[:], True, False, 128)])
+        mm(["i4k", "n4k", "c160", ky], [pk("y")], group(pa("y"), [(T.n4k[:], T.c160[:, 0:H]), (T.i4k[:], Y)]))
         dve(H, [ku], [k_("r16")], cp(T.r16[:, c], U), 0.5)
         for q in range(4):
-            dve(H, gk + [D + ".3"], [k_("d%d" % q)],
-                many([tt(kk(T.d, k), gj(T.gg, k), sl(D, 3), OP.subtract) for k in range(4 * q, 4 * q + 4)]), 1.0, 4)
-            mm([k_("d%d" % q), "pk"] + slots(A), slots(A), [(ps[A][:], T.pk[:, 12 - 4 * q:140 - 4 * q], ch(T.d, q), q == 0, q == 3, 512)])
-        for q in (0, 2):
-            dk = [k_("d%d" % q), k_("d%d" % (q + 1))]
-            dve(1024, dk, [k_("fx%d" % q)], ts(ch(T.fx, q, 2), ch(T.d, q, 2), CX - 160.0 * 4096, CX, OP.add, OP.not_equal), 0.5)
-            act(1024, dk, [k_("ad%d" % q)], af(ch(T.ad, q, 2), ch(T.d, q, 2), AF.Abs, -160.0, 1.0 / 4096))
-            ks = range(4 * q, 4 * q + 8)
-            mm([k_("ad%d" % q), "g8s", C + ".1"], [C + ".1"],
-               [(ps[C][:, H + k:2 * H:16], kk(T.ad, k), T.g8s[:], False, False, 64) for k in ks])
-        act(512, slots(A), [k_("wp")], af(wq, ps[A][:], AF.Identity, -160.0 * 33825))
-        for q in range(4):
-            mm(gk + ["i32"], [B + ".0"], [(ps[B][:, k:H:16], gj(T.gg, k), T.i32[:, (k + t) % 16:128:16], True, True, 256)
-                                          for k in range(4 * q, 4 * q + 4)])
-        act(H, [B + ".0"], [k_("n32")], af(T.n32[:, c], sl(B, 0), AF.Identity))
-        act(H, [B + ".0"], [k_("nr")], af(T.nr[:, c], sl(B, 0), AF.Identity, 128.0, 1.0 / 4096))
-        mm([k_("n32"), k_("nr"), "i32", "n4k"], [B + ".1"],
-           [(sl(B, 1), T.nr[:, c], T.n4k[:], True, False, 128), (sl(B, 1), T.n32[:, c], T.i32[:], False, True, 512)])
-        dve(H, [B + ".1"], [k_("nu")], ts(T.nu[:, c], sl(B, 1), 128.0 * 4096, None, OP.add))
-        dve(H, [k_("nu")], [k_("n16")], cp(T.n16[:, c], T.nu[:, c]), 0.5)
+            dve(H, gk + [pk("y")], [k_("d%d" % q)],
+                many([tt(kk(T.d, s), gj(T.gg, jur(s)), pa("y"), OP.subtract) for s in range(4 * q, 4 * q + 4)]), 1.0, 4)
+        pick = lambda k, whole: (byk("nom", k, 16), gj(T.gg, k), T.i32[:, (k + t) % 16:128:16], whole, whole or k == 15, 256)
+        if CFG["nom"] == 1:
+            for q in range(4):
+                mm(gk + ["i32"], [pk("nom")], [pick(k, True) for k in range(4 * q, 4 * q + 4)])
+            act(H, [pk("nom")], [k_("n32")], af(T.n32[:, c], pa("nom"), AF.Identity))
+            act(H, [pk("nom")], [k_("nr")], af(T.nr[:, c], pa("nom"), AF.Identity, 160.0, 1.0 / 4096))
+            mm([k_("n32"), k_("nr"), "i32", "n4k"], [pk("nt")],
+               [(pa("nt"), T.nr[:, c], T.n4k[:], True, False, 128), (pa("nt"), T.n32[:, c], T.i32[:], False, True, 512)])
+            dve(H, [pk("nt")], [k_("nu")], ts(T.nu[:, c], pa("nt"), 160.0 * 4096, None, OP.add))
+            dve(H, [k_("nu")], [k_("n16")], ts(T.n16[:, c], T.nu[:, c], -2048.0, None, OP.add), 0.5)
+            n16 = (T.ih[:], T.n16[:, c])
+        else:
+            mm(["i4k", "c160"], [pk("nom")], group(pa("nom"), [(T.i4k[:], T.c160[:, 0:H])], True, 128, False))
+            for q in range(4):
+                mm(gk + ["i32", pk("nom")], [pk("nom")], [pick(k, False) for k in range(4 * q, 4 * q + 4)])
+            act(H, [pk("nom")], [k_("nr")], af(T.nr[:, c], pa("nom"), AF.Identity, 0.0, 1.0 / 4096))
+            mm([k_("nr"), "n4k", pk("nom")], [pk("nom")], group(pa("nom"), [(T.n4k[:], T.nr[:, c])], False))
+            dve(H, [pk("nom")], [k_("n16")], ts(T.n16[:, c], pa("nom"), -2048.0, None, OP.add))
+            n16 = (T.n16[:, c], T.ih[:])
+            mm([k_("n16"), "ih"], [pk("nt")], group(pa("nt"), [n16]))
+            dve(H, [pk("nt")], [k_("nu")], ts(T.nu[:, c], pa("nt"), 2048.0, None, OP.add))
         zk = []
-        for e, i0, i1 in GATH_Z[h]:
+        for e, i0, i1 in CFG["gz"][h]:
             src = T.tab[:, 0:2048].indirect(T.nu[:, H * h + i0:H * h + i1])
             out = T.zz[:, q0 + 16 * i0:q0 + 16 * i1]
             zk.append(k_("z%d" % i0))
             if e == "act":
-                act(16 * (i1 - i0), TAB + [k_("nu")], zk[-1:], af(out, src, AF.Identity, 128.0, 1.0 / 4096), GC)
+                act(16 * (i1 - i0), TAB + [k_("nu")], zk[-1:], af(out, src, AF.Identity, 160.0, 1.0 / 4096), GC)
             else:
-                dve(16 * (i1 - i0), TAB + [k_("nu")], zk[-1:], ts(out, src, 1.0 / 4096, 128.0, OP.mult, OP.add), GC)
-        mm([k_("fx0"), k_("fx2"), "ib"], [D + ".0"], group(sl(D, 0), [(T.ib[:], kk(T.fx, k)) for k in range(16)]))
-        act(H, [D + ".0"], [k_("bad")], step(T.bad[:, c], sl(D, 0), 8.5))
-        mm([k_("fx0"), k_("fx2"), "zs"], [B + ".3"], group(sl(B, 3), [(T.zs[:, 15 - k:143 - k], kk(T.fx, k)) for k in range(16)]))
-        act(H, [B + ".3"], [k_("a")], step(T.a[:, c], sl(B, 3), 4.5, -1.0))
-        act(H, [B + ".3"], [k_("pc")], af(T.pc[:, c], sl(B, 3), AF.Identity))
-        mm([k_("bad"), "tri"], [D + ".1"], group(sl(D, 1), [(T.tri[:], T.bad[:, c])]))
-        act(H, [D + ".1", "pm"], [k_("m")], step(T.m[:, c], sl(D, 1), PM))
-        mm([k_("a"), "bo"], [D + ".2"], group(sl(D, 2), [(T.bo[:], T.a[:, c])]))
-        act(H, [D + ".2", "thr"], [k_("nl"), k_("acc")],
-            step(T.nl[:, c], sl(D, 2), T.thr[:, 0:1], 1.0, None if last else T.acc[:, 4 * h:4 * h + 1]))
-        mm([k_("a"), k_("nl"), "ibig", C + ".1"], [C + ".1"],
-           group(sl(C, 1), [(T.a[:, c], T.ibig[:]), (T.nl[:, c], T.ibig[:])], False, 128, False))
-        mm([k_("m"), "fw"], slots(A), [(sl(A, j), T.fw[:], T.m[:, c], True, True, 128) for j in range(4)])
-        dve(512, [k_("wp")] + slots(A), [k_("tp")], tt(tq, wq, ps[A][:], OP.mult))
-        mm([k_("tp"), "sj"], [B + ".2"],
-           [(ps[B][:, 2 * H + j:3 * H:4], T.tp[:, 512 * h + H * j:512 * h + H * (j + 1)], T.sj[:], True, True, 256) for j in range(4)])
-        dve(H, [B + ".2"], [k_("ra")], ts(T.ra[:, c], sl(B, 2), CK, -CK - 160.0, OP.add, OP.add))
-        dve(H, [B + ".2", k_("ra")], [k_("dr")], tt(T.dr[:, c], sl(B, 2), T.ra[:, c], OP.subtract))
-        mm([k_("dr"), "ib", C + ".1"], [C + ".1"], group(sl(C, 1), [(T.ib[:], T.dr[:, c])], False))
-        dve(H, [k_("dr")], [k_("fo")], ts(T.fo[:, c], T.dr[:, c], CD - 160.0, CD, OP.add, OP.not_equal), 0.5)
-        dve(H, [C + ".1", "rst"], [k_("mins")],
-            lambda: ve.tensor_tensor_scan(T.mins[:, c], T.rst[:], sl(C, 1), 131072.0, OP.max, OP.min))
-        mb = lambda: T.mins[:, c].indirect(T.ends[:])
-        dve(H, [k_("mins"), "ends"], [k_("rb")], ts(T.rb[:, c], mb(), CK, -CK, OP.add, OP.add), GC)
-        dve(H, [k_("mins"), "ends", k_("rb")], [k_("dbc")], tt(T.dbc[:, c], mb(), T.rb[:, c], OP.subtract), GC)
-        mm([k_("dbc"), "ib"], [D + ".3"], group(sl(D, 3), [(T.dbc[:, c], T.ib[:])]))
-        mm([k_("dbc"), k_("dr"), "ib", "nib"], [C + ".0"], group(sl(C, 0), [(T.ib[:], T.dr[:, c]), (T.nib[:], T.dbc[:, c])]))
-        dve(H, [D + ".3", k_("m")], [D + ".3"], tt(sl(D, 3), T.m[:, c], sl(D, 3), OP.mult))
-        dve(H, [D + ".3", ky], [kyn], tt(YN, Y, sl(D, 3), OP.add))
+                dve(16 * (i1 - i0), TAB + [k_("nu")], zk[-1:], ts(out, src, 1.0 / 4096, 160.0, OP.mult, OP.add), GC)
+        for q in range(4):
+            mm([k_("d%d" % q)] + ["dig%d" % j for j in range(4)], ["%s.%d" % (A, q)],
+               group(sl(A, q), [(T.dig[:, H * j:H * j + H], kk(T.d, 4 * q + j)) for j in range(4)]))
+        mm(["ib", "ini1"], [pk("key")], group(pa("key"), [(T.ib[:], T.ini[:])], True, 128, False))
+        for q in (0, 2):
+            dk = [k_("d%d" % q), k_("d%d" % (q + 1))]
+            dve(1024, dk, [k_("fx%d" % q)], ts(ch(T.fx, q, 2), ch(T.d, q, 2), CX - 160.0 * 4096, CX, OP.add, OP.not_equal), 0.5)
+            act(1024, dk, [k_("ad%d" % q)], af(ch(T.ad, q, 2), ch(T.d, q, 2), AF.Abs, -160.0, 1.0 / 4096))
+            mm([k_("ad%d" % q), "g8s", pk("key")], [pk("key")],
+               [(byk("key", jur(s), 16), kk(T.ad, s), T.g8s[:], False, False, 64) for s in range(4 * q, 4 * q + 8)])
+        for q in (0, 2):
+            mm([k_("fx%d" % q)] + WFK + ([pk("v")] if q else []), [pk("v")],
+               group(pa("v"), [(T.wf[:, H * jur(s):H * jur(s) + H], kk(T.fx, s)) for s in range(4 * q, 4 * q + 8)], q == 0, 128, q == 2))
+        act(H, [pk("v")], [k_("bad")], af(T.bad[:, c], pa("v"), AF.Identity, 128.0 + 15.0 / 64, 1.0 / 32))
+        act(H, [pk("v")], [k_("pc")], af(T.pc[:, c], pa("v"), AF.Identity, 127.75, 1.0 / 32))
+        act(H, [pk("v")], [k_("a")], step(T.a[:, c], pa("v"), 152.0, -1.0))
+        mm([k_("bad"), k_("pc"), "tri", "ntri"], [pk("tri")], group(pa("tri"), [(T.tri[:], T.bad[:, c]), (T.ntri[:], T.pc[:, c])]))
+        act(H, [pk("tri"), "pm"], [k_("m")], step(T.m[:, c], pa("tri"), PM))
+        mm([k_("a"), "bo"], [pk("c")], group(pa("c"), [(T.bo[:], T.a[:, c])]))
+        act(H, [pk("c"), "thr"], [k_("nl"), k_("acc")],
+            step(T.nl[:, c], pa("c"), T.thr[:, 0:1], 1.0, None if last else T.acc[:, 4 * h:4 * h + 1]))
+        mm([k_("a"), k_("nl"), "ibig", pk("key")], [pk("key")],
+           group(pa("key"), [(T.a[:, c], T.ibig[:]), (T.nl[:, c], T.ibig[:])], False, 128, False))
+        tq = lambda q: T.tp[:, 512 * h + H * q:512 * h + H * (q + 1)]
+        for q in (0, 2):
+            dve(H, [k_("m"), "%s.%d" % (A, q), "%s.%d" % (A, q + 1)], [k_("tp%d" % q)],
+                many([tt(tq(j), T.m[:, c], sl(A, j), OP.mult) for j in (q, q + 1)]), 1.0, 2)
+            calls = [(byk("dr", j, 4), tq(j), T.sj[:], False, j == 3, 256) for j in (q, q + 1)]
+            if q == 0:
+                calls = [(pa("dr"), T.ib[:], T.cw[:], True, False, 128)] + calls
+            mm([k_("tp%d" % q), "ib", "cw"] + SJ + ([pk("dr")] if q else []), [pk("dr")], calls)
+        dve(H, [pk("dr")], [k_("ra")], ts(T.ra[:, c], pa("dr"), CK, -CK - 160.0, OP.add, OP.add))
+        dve(H, [pk("dr"), k_("ra")], [k_("dr")], tt(T.dr[:, c], T.ra[:, c], pa("dr"), OP.subtract))
+        mm([k_("dr"), "nib", pk("key")], [pk("key")], group(pa("key"), [(T.nib[:], T.dr[:, c])], False))
+        dve(H, [k_("dr")], [k_("fo")], ts(T.fo[:, c], T.dr[:, c], CD + 160.0, CD, OP.add, OP.not_equal), 0.5)
+        dve(H, [pk("key"), "rst"], [k_("mins")],
+            lambda: ve.tensor_tensor_scan(T.mins[:, c], T.rst[:], pa("key"), 131072.0, OP.max, OP.min))
+        me, rb, db = T.mins[:, H * h + 15:H * h + H:16], T.rb[:, 8 * h:8 * h + 8], T.db[:, 16 * h:16 * h + 8]
+        dve(8, [k_("mins")], [k_("rb")], ts(rb, me, CK, -CK, OP.add, OP.add))
+        dve(8, [k_("mins"), k_("rb")], [k_("db")], tt(db, me, rb, OP.subtract))
+        dve(H, [k_("db"), "ends"], [k_("dbc")], cp(T.dbc[:, c], db.indirect(T.ends[:])), GC)
+        mm([k_("dbc"), "ib"], [pk("dl")], group(pa("dl"), [(T.dbc[:, c], T.ib[:])]))
+        mm([k_("dbc"), k_("dr"), "ib"], [pk("dn")], group(pa("dn"), [(T.ib[:], T.dr[:, c]), (T.ib[:], T.dbc[:, c])]))
+        dve(H, [pk("dl"), k_("m")], [pk("dl")], tt(pa("dl"), T.m[:, c], pa("dl"), OP.mult))
+        dve(H, [pk("dl"), ky], [kyn], tt(YN, Y, pa("dl"), OP.add))
         send([kyn], ["yi%d%d" % (t + 1, h)], T.yi[:, o1:o1 + H], YN)
-        dve(H, [C + ".0"], [k_("fn")], ts(T.fn[:, c], sl(C, 0), CD - 160.0, CD, OP.add, OP.not_equal))
-        mm([k_("fn"), k_("fo"), k_("pc"), "ib", "nib"], [C + ".2"],
-           group(sl(C, 2), [(T.ib[:], T.pc[:, c]), (T.fo[:, c], T.nib[:]), (T.fn[:, c], T.ib[:])]))
-        act(H, [C + ".2"], [k_("a2")], step(T.a2[:, c], sl(C, 2), 4.5, -1.0))
-        mm([k_("a2"), "w2"], [D + ".2"], group(sl(D, 2), [(T.w2[:], T.a2[:, c])]))
-        act(H, [D + ".2"], [k_("wa")], step(T.wa[:, c], sl(D, 2), 27.5))
-        mm([k_("wa"), "i16"], [C + ".3", C + ".1"], group(sl(C, 3), [(T.wa[:, c], T.i16[:])], True, 128, False))
+        dve(H, [pk("dn")], [k_("fn")], ts(T.fn[:, c], pa("dn"), CD + 160.0, CD, OP.add, OP.not_equal))
+        mm([k_("fn"), k_("fo"), k_("pc"), "ib", "nib"], [pk("a2")],
+           group(pa("a2"), [(T.ib[:], T.pc[:, c]), (T.fo[:, c], T.nib[:]), (T.fn[:, c], T.ib[:])]))
+        act(H, [pk("a2")], [k_("a2")], step(T.a2[:, c], pa("a2"), 132.5, -1.0))
+        mm([k_("a2"), "w2"], [pk("w2")], group(pa("w2"), [(T.w2[:], T.a2[:, c])]))
+        act(H, [pk("w2")], [k_("wa")], step(T.wa[:, c], pa("w2"), 27.5))
+        mm([k_("a2"), "w1"], [pk("w1")], group(pa("w1"), [(T.w1[:], T.a2[:, c])]))
+        dve(H, [pk("w1")], [k_("m1")], ts(T.m1[:, c], pa("w1"), CM, CM + 8.0, OP.add, OP.not_equal))
+        if "dve" in CFG["zs"][h]:
+            mm([kyn, "ib"], [pk("yn")], group(pa("yn"), [(T.ib[:], YN)]))
+        mm([kyn, "wh", "wl"], [pk("u")], group(pa("u"), [(T.wh[:], YN), (T.wl[:], YN)]))
+        dve(H, [pk("u")], [k_("ur")], ts(T.ur[:, c], pa("u"), 1.0 / 2048, 1024.5 + 2.0 ** -12, OP.mult, OP.add))
+        mm([kyn, "wh", "wl", "wu", "cu", "n2h", k_("ur")], [pk("u")],
+           group(pa("u"), [(T.wh[:], YN), (T.wl[:], YN), (T.wu[:], T.cu[:]), (T.n2h[:], T.ur[:, c])]))
+        dve(H, [pk("u"), k_("r16")], [k_("pp")], tt(T.pp[:, c], T.r16[:, c], pa("u"), OP.mult))
+        dve(H, [k_("pp"), "pfar"], [k_("pq")], ts(T.pq[:, c], T.pp[:, c], PF, None, OP.add))
+        dve(H, [k_("pq")], [k_("far")], ts(T.far[:, c], T.pq[:, c], 5, 2047, OP.arith_shift_right, OP.bitwise_and))
         if h == 1:
-            at = ps[D][:, H:H + 16]
-            mm(["yq%d0" % t, kyn, "zw"], [D + ".1"],
-               group(at, [(T.zw[:, 15 - j:143 - j], T.yq[:, 256 * t + j:256 * t + 256:16]) for j in range(16)], True, 64))
-            dve(16, [D + ".1"], ["ca"], cp(T.ca[:], at))
+            b, c0, key = at("col")
+            w = ps[b][:, c0:c0 + 16]
+            mm(["yq%d0" % t, kyn, "zw"], [key],
+               group(w, [(T.zw[:, 15 - j:143 - j], T.yq[:, 256 * t + j:256 * t + 256:16]) for j in range(16)], True, 64))
+            dve(16, [key], ["ca"], cp(T.ca[:], w))
             dve(16, ["ca"], ["cb"], ts(T.cb[:], T.ca[:], 7, None, OP.bitwise_and))
             dve(16, ["cb", "base0"], ["cc"], tt(T.cc[:], T.cb[:], T.base[:], OP.add))
             dve(16, ["cc"], ["col"], cp(T.col[:], T.cc[:]))
+        mm([k_("n16"), k_("m1"), "ih", "i4k"], [pk("p1")], group(pa("p1"), [n16, (T.i4k[:], T.m1[:, c])]))
+        dve(H, [pk("p1"), k_("r16")], [k_("t1")], tt(T.t1[:, c], T.r16[:, c], pa("p1"), OP.min))
+        turn = 0
         for q in range(4):
-            b = (B, A)[q % 2]
-            calls = []
-            for j in range(4):
-                calls += group(sl(b, j), [(T.ib[:], gj(T.zz, 4 * q + j)), (T.nib[:], YN)])
-            mm(zk + [kyn, "ib", "nib"], slots(b), calls)
-            if q in FZ_ACT[h]:
-                act(512, slots(b), [k_("az%d" % q)], af(ch(T.az, q), ps[b][:], AF.Abs, -128.0))
-                dve(512, [k_("az%d" % q)], [k_("fz%d" % q)], ts(ch(T.fz, q), ch(T.az, q), 2.5, None, OP.is_gt), 0.5)
+            if CFG["zs"][h][q] != "dve":
+                b = (B, A)[turn % 2]
+                turn += 1
+                calls = []
+                for j in range(4):
+                    calls += group(sl(b, j), [(T.ib[:], gj(T.zz, 4 * q + j)), (T.nib[:], YN)])
+                mm(zk + [kyn, "ib", "nib"], slots(b), calls)
+                if CFG["zs"][h][q] == "pe":
+                    dve(512, slots(b), [k_("fz%d" % q)], ts(ch(T.fz, q), ps[b][:], CD - 160.0, CD, OP.add, OP.not_equal))
+                else:
+                    act(512, slots(b), [k_("dz%d" % q)], af(ch(T.dz, q), ps[b][:], AF.Abs, -160.0))
+                    dve(512, [k_("dz%d" % q)], [k_("fz%d" % q)], ts(ch(T.fz, q), ch(T.dz, q), 2.5, None, OP.is_gt), 0.5)
             else:
-                dve(512, slots(b), [k_("fz%d" % q)], ts(ch(T.fz, q), ps[b][:], CD - 128.0, CD, OP.add, OP.not_equal))
-            mm([k_("fz%d" % q), "g8", C + ".3"], [C + ".3"],
-               [(ps[C][:, 3 * H + k:4 * H:16], kk(T.fz, k), T.g8[:], False, k == 15, 64) for k in range(4 * q, 4 * q + 4)])
-        uw = [(T.wh[:], YN), (T.wl[:], YN)]
-        mm([kyn, "wh", "wl", "ih", "cu"], [D + ".0"], group(sl(D, 0), [(T.ih[:], T.cu[:])] + uw))
-        dve(H, [D + ".0"], [k_("ur")], ts(T.ur[:, c], sl(D, 0), CU, -CU, OP.add, OP.add))
-        mm([kyn, "wh", "wl", "ih", "c32", "nib", k_("ur")], [D + ".1"],
-           group(sl(D, 1), [(T.ih[:], T.c32[:])] + uw + [(T.nib[:], T.ur[:, c])]))
-        dve(H, [D + ".1", k_("r16")], [k_("pp")], tt(T.pp[:, c], T.r16[:, c], sl(D, 1), OP.mult))
-        dve(H, [k_("pp"), "pfar"], [k_("pq")], ts(T.pq[:, c], T.pp[:, c], PF, None, OP.add))
-        dve(H, [k_("pq")], [k_("far")], ts(T.far[:, c], T.pq[:, c], 5, 2047, OP.arith_shift_right, OP.bitwise_and))
-        mm([k_("n16"), "ih"], [D + ".2"], group(sl(D, 2), [(T.ih[:], T.n16[:, c])]))
-        dve(H, [k_("far"), D + ".2"], [k_("fmn")], tt(T.fmn[:, c], T.far[:, c], sl(D, 2), OP.subtract))
-        mm([k_("a2"), "w1"], [D + ".0"], group(sl(D, 0), [(T.w1[:], T.a2[:, c])]))
-        dve(H, [D + ".0"], [k_("m1")], ts(T.m1[:, c], sl(D, 0), CM, CM + 8.0, OP.add, OP.is_equal))
-        mm([k_("n16"), k_("r16"), "ih", "nih"], [D + ".1"], group(sl(D, 1), [(T.ih[:], T.n16[:, c]), (T.nih[:], T.r16[:, c])]))
-        dve(H, [D + ".1", k_("m1")], [k_("t1")], tt(T.t1[:, c], T.m1[:, c], sl(D, 1), OP.mult))
-        act(H, [C + ".3"], [k_("tf")], step(T.tf[:, c], sl(C, 3), 20.5))
-        mm([k_("tf"), "ib"], [D + ".2"], group(sl(D, 2), [(T.tf[:, c], T.ib[:])]))
-        parts = [T.r16[:, c], T.t1[:, c], T.hh[:, c]]
-        pk = [k_("r16"), k_("t1"), k_("hh")]
+                dve(H, zk + [pk("yn")], [k_("dz%d" % q)],
+                    many([tt(kk(T.dz, k), gj(T.zz, k), pa("yn"), OP.subtract) for k in range(4 * q, 4 * q + 4)]), 1.0, 4)
+                dve(512, [k_("dz%d" % q)], [k_("fz%d" % q)], ts(ch(T.fz, q), ch(T.dz, q), CD - 160.0, CD, OP.add, OP.not_equal), 0.5)
+        mm([k_("wa"), "i16"], [pk("tf")], group(pa("tf"), [(T.wa[:, c], T.i16[:])], True, 128, False))
+        for q in range(4):
+            mm([k_("fz%d" % q), "g8", pk("tf")], [pk("tf")],
+               [(byk("tf", k, 16), kk(T.fz, k), T.g8[:], False, k == 15, 64) for k in range(4 * q, 4 * q + 4)])
+        act(H, [pk("tf")], [k_("tf")], step(T.tf[:, c], pa("tf"), 20.5))
+        mm([k_("t1"), k_("m1"), k_("tf"), "ih", "n2k", "i4k"], [pk("p2")],
+           group(pa("p2"), [(T.ih[:], T.t1[:, c]), (T.n2k[:], T.m1[:, c]), (T.tf[:, c], T.i4k[:])]))
         if not last:
-            mm(pk[:2] + ["ih", "i4k", kyn], [D + ".0"], group(sl(D, 0), [(T.i4k[:], YN)] + [(T.ih[:], p) for p in parts[:2]]))
-            act(H, [D + ".0"], [k_("cn")], af(T.cn[:, c], sl(D, 0), AF.Identity))
-            dve(H, [D + ".2", k_("fmn")], [k_("hh")], tt(T.h32[:, c], T.fmn[:, c], sl(D, 2), OP.mult))
-            mm(pk + ["ih", "i32"], [D + ".3"],
-               group(sl(D, 3), [(T.ih[:], p) for p in parts[:2]], True, 128, False) + [(sl(D, 3), T.i32[:], T.h32[:, c], False, True, 512)])
-            dve(H, [D + ".3"], ["uq%d%d" % (t, h)], cp(T.uq[:, o0:o0 + H], sl(D, 3)))
-            send(["uq%d%d" % (t, h)], ["ui%d%d" % (t + 1, h)], T.ui[:, o1:o1 + H], T.uq[:, o0:o0 + H])
+            kuq = "uq%d%d" % (t, h)
+            dve(H, [pk("p2"), k_("far")], [k_("t2")], tt(T.t2[:, c], T.far[:, c], pa("p2"), OP.min))
+            mm([kyn, k_("tf"), "i4k", "n2k"], [pk("cn")], group(pa("cn"), [(T.i4k[:], YN), (T.tf[:, c], T.n2k[:])]))
+            act(H, [pk("cn")], [k_("cn")], af(T.cn[:, c], pa("cn"), AF.Identity, 2048.0))
+            mm([k_("t2"), k_("tf"), "n2k", "i32"], [pk("uq")],
+               [(pa("uq"), T.tf[:, c], T.n2k[:], True, False, 128), (pa("uq"), T.i32[:], T.t2[:, c], False, True, 512)])
+            dve(H, [pk("uq")], [kuq], ts(T.uq[:, o0:o0 + H], pa("uq"), 2048.0, None, OP.add))
+            send([kuq], ["ui%d%d" % (t + 1, h)], T.ui[:, o1:o1 + H], T.uq[:, o0:o0 + H])
+            if CFG["yz"] == "inc":
+                dve(H, [kuq], [k_("w16")], cp(T.w16[:, c], T.uq[:, o0:o0 + H]), 0.5)
+                mm([k_("w16"), "wz"], [pk("yz")], group(pa("yz"), [(T.wz[:], T.w16[:, c])]))
+                act(H, [pk("yz")], [k_("sy")], af(T.sy[:, c], pa("yz"), AF.Identity))
         else:
-            dve(H, [D + ".2", k_("fmn")], [k_("hh")], tt(T.hh[:, c], T.fmn[:, c], sl(D, 2), OP.mult))
-            mm(pk + ["ih"], [D + ".3"], group(sl(D, 3), [(T.ih[:], p) for p in parts]))
-            mm(pk + ["wz"], [B + ".0"], group(sl(B, 0), [(T.wz[:], p) for p in parts]))
-            dve(H, [D + ".3"], [k_("rq")], cp(T.rq[:, c], sl(D, 3)))
+            dve(H, [pk("p2"), k_("far")], [k_("t2")], tt(T.t2h[:, c], T.far[:, c], pa("p2"), OP.min))
+            mm([k_("t2"), k_("tf"), "n2k", "ih"], [pk("uq")], group(pa("uq"), [(T.tf[:, c], T.n2k[:]), (T.ih[:], T.t2h[:, c])]))
+            act(H, [pk("uq")], [k_("rq")], af(T.rq[:, c], pa("uq"), AF.Identity, 2048.0))
             send([k_("rq")], [k_("ri")], T.ri[:, c], T.rq[:, c])
-            act(H, [B + ".0"], [k_("cn")], af(T.cn[:, c], sl(B, 0), AF.Identity))
+            mm([k_("rq"), "wz32"], [pk("yz")], group(pa("yz"), [(T.wz32[:], T.rq[:, c])], True, 512))
+            act(H, [pk("yz")], [k_("sy")], af(T.sy[:, c], pa("yz"), AF.Identity))
+
+    def sums(q, b):
+        s = slice(512 * q, 512 * q + 512)
+        if CFG["hx"][q] == "act":
+            act(512, TAB, ["hx%d" % q], af(T.hx[:, s], T.tab[:, s], AF.Identity, 160.0, 1.0 / 4096))
+            terms = [(T.wz4[:], T.hx[:, s]), (T.wz4[:], T.c160[:])]
+            assert False
+        else:
+            dve(512, TAB, ["hx%d" % q], ts(T.hx[:, s], T.tab[:, s], 1.5 * 2 ** 35, -1.5 * 2 ** 35, OP.add, OP.add))
+            terms = [(T.nwz[:], T.hx[:, s])]
+        mm(TAB + ["hx%d" % q, "nwz", "wz32"], slots(b),
+           group(ps[b][:], terms, True, 512, False) + [(ps[b][:], T.wz32[:], T.tab[:, s], False, True, 2048)])
+        act(512, slots(b), ["yzt%d" % q], af(T.yzt[:, s], ps[b][:], AF.Identity))
 
     YZ = ["yzt%d" % q for q in range(4)]
     for t in range(V):
-        visit[0] = t
+        if t == V - 1 and CFG["yz"] != "inc":
+            for q in range(4):
+                sums(q, ("A1", "C1")[q % 2])
         half(t, 0)
         half(t, 1)
         for h in (0, 1):
-            c, at = slice(H * h, H * h + H), T.col[:, 8 * h:8 * h + 8]
+            c, w = slice(H * h, H * h + H), T.col[:, 8 * h:8 * h + 8]
+            s = slice(1024 * h, 1024 * h + 1024)
             if t < V - 1:
-                dve(H, ["cn_%d" % h, "hh_%d" % h, "col"] + TAB, TAB,
-                    tt(T.tab[:, 0:2048].indirect(at), T.cn[:, c], T.h32[:, c], OP.add), SC)
-            else:
-                dve(H, ["cn_%d" % h, "col"] + YZ, YZ, cp(T.yzt[:, 0:2048].indirect(at), T.cn[:, c]), SC)
+                dve(H, ["cn_%d" % h, "t2_%d" % h, "col"], TAB[2 * h:2 * h + 2],
+                    tt(T.tab[:, s].indirect(w), T.cn[:, c], T.t2[:, c], OP.add), SC)
+            if t == V - 1 or CFG["yz"] == "inc":
+                dve(H, ["sy_%d" % h, "col"] + YZ[2 * h:2 * h + 2], YZ[2 * h:2 * h + 2], cp(T.yzt[:, s].indirect(w), T.sy[:, c]), SC)
         if t < V - 1:
             mm(["acc_0", "acc_1", "o16"], ["A1.1"], [(ps["A1"][:, H:H + 1], T.o16[:], T.acc[:, 4 * h:4 * h + 1], h == 0, h == 1, 256)
                                                      for h in (0, 1)])
@@ -471,10 +504,11 @@ def order(ops):
             readers[k] = []
     n = len(ops)
     cost = [o["cost"] for o in ops]
-    hold = [o["cost"] if o["kind"] == "c" else 0.1 for o in ops]
+    hold = [o["cost"] if o["kind"] == "c" else (0.3 if o["kind"] == "send" else 0.1) for o in ops]
     eng = [o["eng"] for o in ops]
     pred = [[(p, 0.0 if eng[p] == eng[i] and ops[p]["kind"] == "c" and (p not in o["raw"] or eng[i] == "pe") else LAT)
              for p in sorted(o["raw"] | o["oth"])] for i, o in enumerate(ops)]
+    uses = [[o["eng"]] + o["banks"] for o in ops]
     back = [[] for _ in ops]
     for i in range(n):
         for p, gap in pred[i]:
@@ -483,33 +517,46 @@ def order(ops):
     def place(keys, before, after, turned):
         left = [len(b) for b in before]
         ready = [i for i in range(n) if left[i] == 0]
-        start, busy = [0.0] * n, {}
+        start, free = [0.0] * n, [0.0] * n
+        busy = {r: [] for u in uses for r in u}
         while ready:
-            i = min(ready, key=lambda x: keys[x])
+            i = min(ready, key=keys.get)
             ready.remove(i)
-            s = max([start[p] + cost[p] + gap for p, gap in before[i]] or [0.0])
             lead = cost[i] - hold[i] if turned else 0.0
-            moved = True
-            while moved:
-                moved = False
-                for r in [eng[i]] + ops[i]["banks"]:
-                    for a, b, e in reversed(busy.get(r, ())):
-                        pad = 0.0 if e == eng[i] else LAT
-                        if b + pad <= s + lead - 6.0:
-                            break
-                        if a - pad < s + lead + hold[i] - 1e-9 and b + pad > s + lead + 1e-9:
-                            s = b + pad - lead
-                            moved = True
-            start[i] = s
-            for r in [eng[i]] + ops[i]["banks"]:
-                lst = busy.setdefault(r, [])
-                lst.append((s + lead, s + lead + hold[i], eng[i]))
-                j = len(lst) - 1
-                while j > 0 and lst[j - 1][0] > lst[j][0]:
-                    lst[j - 1], lst[j] = lst[j], lst[j - 1]
+            s, e, w = free[i] + lead, eng[i], hold[i]
+            calm = False
+            while not calm:
+                calm = True
+                for r in uses[i]:
+                    lst = busy[r]
+                    lo, hi = 0, len(lst)
+                    while lo < hi:
+                        mid = (lo + hi) // 2
+                        if lst[mid][1] + LAT <= s:
+                            lo = mid + 1
+                        else:
+                            hi = mid
+                    for a, b, x in lst[lo:lo + 40]:
+                        pad = 0.0 if x == e else LAT
+                        if a - pad >= s + w - 1e-9:
+                            if a - LAT >= s + w:
+                                break
+                        elif b + pad > s + 1e-9:
+                            s = b + pad
+                            calm = False
+            for r in uses[i]:
+                lst = busy[r]
+                j = len(lst)
+                while j > 0 and lst[j - 1][0] > s:
                     j -= 1
+                lst.insert(j, (s, s + w, e))
+            s -= lead
+            start[i] = s
+            s += cost[i]
             for x, gap in after[i]:
                 left[x] -= 1
+                if s + gap > free[x]:
+                    free[x] = s + gap
                 if left[x] == 0:
                     ready.append(x)
         return start, max(start[i] + cost[i] for i in range(n))
@@ -518,25 +565,28 @@ def order(ops):
         tail = [0.0] * n
         for i in range(n - 1, -1, -1):
             tail[i] = cost[i] + max([tail[x] + gap for x, gap in back[i]] or [0.0])
-        def by(ranking):
-            keys = [0.0] * n
-            for i in range(n - 1, -1, -1):
-                if ops[i]["cls"] is not None:
-                    keys[i] = 1000.0 * ops[i]["at"] + ranking.get(ops[i]["cls"], 0.0)
-                elif ops[i]["kind"] == "dma" and ops[i]["at"] < 0:
-                    keys[i] = i - 1.0e6
-                else:
-                    keys[i] = min([keys[x] for x, gap in back[i]] or [1.0e6]) - cost[i]
-            return place(keys, pred, back, False)
-        MEMO["by"], MEMO["tail"] = by, tail
-        MEMO["start"] = by({k: float(j) for j, k in enumerate(RANKING.split())}) if RANKING else \
-            place([-v for v in tail], pred, back, False)
+        first = lambda keys: {i: i - 1.0e6 if ops[i]["kind"] == "dma" and not pred[i] else keys[i] for i in range(n)}
+
+        def tighten(now):
+            late = place({i: -(now[0][i] + cost[i]) for i in range(n)}, back, pred, True)
+            return place(first([-(late[0][i] + cost[i]) for i in range(n)]), pred, back, False)
+        best = now = tighten(place(first([-v for v in tail]), pred, back, False))
+        rng = np.random.RandomState(CFG["seed"])
+        for j in range(CFG["passes"]):
+            shake = rng.rand(n) * CFG["shake"]
+            lo = rng.rand() * now[1] - 0.5 * CFG["span"]
+            new = tighten(place(first([now[0][i] + (shake[i] if lo < now[0][i] < lo + CFG["span"] else 0.5 * CFG["shake"])
+                                       for i in range(n)]), pred, back, False))
+            if new[1] < now[1] + CFG["slack"]:
+                now = new
+            if now[1] < best[1]:
+                best = now
+        MEMO["start"] = best
     start, end = MEMO["start"]
     seq = sorted(range(n), key=lambda i: (start[i], i))
     bank = {}
     for i in seq:
         o = ops[i]
-        o["start"] = start[i]
         o["bk"] = set(bank[b][e] for b in o["banks"] for e in bank.get(b, {}) if e != eng[i])
         for b in o["banks"]:
             bank.setdefault(b, {})[eng[i]] = i

import numpy as np
from concourse.mybir import AluOpType as OP, ActivationFunctionType as AF

V = 4
H = 128
F32, BF, F16, I32, U16 = "float32", "bfloat16", "float16", "int32", "uint16"


def _sb(n, d):
    return ("sbuf", [128, n], d)


SCRATCH = {
    "xin": _sb(2048, BF), "lin": _sb(2048, I32), "jin": _sb(256, I32), "win": _sb(8, I32), "tab": _sb(2048, F32),
    "hx": _sb(2048, BF), "yzt": _sb(2048, F32),
    "yi": _sb(256 * 5, BF), "ui": _sb(256 * 4, U16), "yq": _sb(256 * 4, BF), "uq": _sb(256 * 3, U16),
    "rq": _sb(256, F32), "ri": _sb(256, F32),
    "gg": _sb(4096, F32), "zz": _sb(4096, BF), "d": _sb(4096, BF), "fx": _sb(4096, BF), "ad": _sb(4096, BF),
    "fz": _sb(4096, BF), "dz": _sb(4096, BF), "tp": _sb(1024, F32),
    "dif": _sb(128, F32), "gm": _sb(128, F32), "g4": _sb(32, F32), "zc": _sb(144, F32),
    "pi": _sb(8, I32), "pj": _sb(8, I32), "pf": _sb(32, F32),
    "i32": _sb(128, F32), "ib": _sb(128, BF), "ih": _sb(128, F16), "n2h": _sb(128, F16), "nib": _sb(128, BF), "bo": _sb(128, BF),
    "i4k": _sb(128, BF), "n4k": _sb(128, BF), "n2k": _sb(128, BF), "ibig": _sb(128, BF), "i16": _sb(128, BF),
    "tri": _sb(128, BF), "ntri": _sb(128, BF), "tmp": _sb(128, BF), "dig": _sb(512, BF), "wf": _sb(2048, BF),
    "w1": _sb(128, BF), "w2": _sb(128, BF), "zs": _sb(144, BF), "zt": _sb(144, BF), "zw": _sb(144, BF),
    "g8s": _sb(8, BF), "g8": _sb(8, BF), "wh": _sb(128, BF), "wl": _sb(128, BF), "wz": _sb(128, F16), "wz32": _sb(128, F32),
    "wz4": _sb(128, BF), "nwz": _sb(128, BF), "c160": _sb(512, BF), "cu": _sb(128, BF), "wu": _sb(128, BF), "cw": _sb(128, BF),
    "sj": _sb(32, F32),
    "ini": _sb(128, BF), "rst": _sb(128, F32), "o16": _sb(128, F32), "ends": _sb(8, U16), "endi": _sb(8, I32),
    "base": _sb(16, I32), "wcol": _sb(16, F32), "wcb": _sb(16, BF),
    "r16": _sb(256, F16), "n32": _sb(256, F32), "nr": _sb(256, BF), "nu": _sb(256, U16), "n16": _sb(256, F16),
    "a": _sb(256, BF), "pc": _sb(256, BF), "nl": _sb(256, BF), "bad": _sb(256, BF), "m": _sb(256, BF), "fo": _sb(256, BF), "fn": _sb(256, BF),
    "ra": _sb(256, F32), "dr": _sb(256, BF), "mins": _sb(256, F32), "rb": _sb(16, F32), "db": _sb(32, BF), "dbc": _sb(256, BF),
    "a2": _sb(256, BF), "m1": _sb(256, BF), "wa": _sb(256, BF), "tf": _sb(256, BF), "ur": _sb(256, F16), "pp": _sb(256, F32),
    "pq": _sb(256, I32), "far": _sb(256, I32), "t1": _sb(256, F16), "t2": _sb(256, F32), "t2h": _sb(256, F16),
    "cn": _sb(256, F32), "w16": _sb(256, F16), "sy": _sb(256, F32),
    "ca": _sb(16, I32), "cb": _sb(16, I32), "cc": _sb(16, I32), "col": _sb(16, U16),
    "acc": _sb(8, F32), "ai": _sb(8, I32), "aj": _sb(8, I32), "thr": _sb(8, F32),
}
BANKS = ("A0", "A1", "B0", "B1", "C0", "C1", "D0", "D1")
for _b in BANKS:
    SCRATCH["ps" + _b] = ("psum", [128, 512], F32)

SEMAPHORES = (["cpe", "cact", "cdve", "cpool", "sent"] + ["dm%d" % i for i in range(16)]
              + ["ar%d" % i for i in range(16)])

CFG = {
    "gx": [[("act", 0, 64), ("dve", 64, 128)], [("act", 0, 64), ("act", 64, 128)]],
    "gz": [[("act", 0, 64), ("act", 64, 128)]] * 2,
    "zs": [["dve", "pe", "pe", "pe"], ["dve", "pe", "pe", "pe"]],
    "nom": 1, "yz": "inc", "hx": ["dve", "act", "dve", "act"],
    "at": {"y": "D3", "nom": "B0", "nt": "B1", "v": "D0", "tri": "D1", "c": "D2", "key": "C1", "dr": "B2", "dl": "D3",
           "dn": "C0", "a2": "C2", "w2": "D2", "tf": "C3", "col": "D1", "u": "D0", "w1": "D1", "p1": "D1", "p2": "D2",
           "cn": "D0", "uq": "D3", "yz": "B0", "yn": "D3"},
    "passes": 1500, "seed": 1, "shake": 2.0, "span": 6.0, "slack": 0.05,
}
COST = {"cyc": 0.00083, "pec": 0.000417, "lat": 0.12, "gc": 1.55, "sc": 3.8, "net": 2.4, "ind": 0.055}
MEMO = {}


def plan(g, core, T, topo):
    rank, n = T.rank_of(core), len(T.cores)
    nxt = T.cores[(rank + 1) % n]
    rid, pid = topo.addr(nxt, core)
    mask = topo.mask(core, nxt)
    nen = len(topo.engines(core, nxt))
    ve, ac, pe = g.vector, g.scalar, g.tensor
    CYC, PEC, GC, SC, NET, IND = [COST[k] for k in ("cyc", "pec", "gc", "sc", "net", "ind")]
    ops = []

    def op(eng, cost, reads, writes, emit, kind="c"):
        banks = sorted(set(k[:2] for k in list(reads) + list(writes) if len(k) == 4 and k[2] == "."))
        ops.append({"eng": eng, "cost": cost, "r": list(reads), "w": list(writes), "emit": emit, "kind": kind, "banks": banks})

    def price(n_el, f):
        return (IND if f in (GC, SC) else 0.0) + max(64, n_el * f) * CYC

    def dve(n_el, reads, writes, emit, f=1.0, calls=1):
        op("dve", calls * price(n_el, f), reads, writes, emit)

    def act(n_el, reads, writes, emit, f=1.0):
        op("act", price(n_el, f), reads, writes, emit)

    def many(emits):
        def emit():
            last = None
            for e in emits:
                last = e()
            return last
        return emit

    def mm(reads, writes, calls, more=False):
        reads, writes = list(reads), list(writes)
        for b in sorted(set(k[:2] for k in writes if len(k) == 4 and k[2] == ".")):
            if calls[0][3] and calls[-1][4] and not more:
                reads.append(b + ".o")
            else:
                writes.append(b + ".o")
        op("pe", sum(c[5] * PEC for c in calls), reads, writes,
           many([(lambda c=c: pe.matmul(c[0], c[1], c[2], c[3], c[4])) for c in calls]))

    def group(out, terms, start=True, cyc=128, stop=True):
        return [(out, w, x, start and j == 0, stop and j == len(terms) - 1, cyc) for j, (w, x) in enumerate(terms)]

    def ts(out, in0, s1, s2, o0, o1=None):
        if o1 is None:
            return lambda: ve.tensor_scalar(out, in0, s1, None, o0)
        return lambda: ve.tensor_scalar(out, in0, s1, s2, o0, o1)

    def tt(out, in0, in1, o):
        return lambda: ve.tensor_tensor(out, in0, in1, o)

    def cp(out, in_):
        return lambda: ve.tensor_copy(out, in_)

    def af(out, in_, func, bias=0.0, scale=1.0, accum=None):
        if accum is None:
            return lambda: ac.activation(out, in_, func, bias, scale)
        return lambda: ac.activation(out, in_, func, bias, scale, accum_out=accum)

    def step(out, in_, at, sign=1.0, accum=None):
        bias = -1000.0 * sign * at if isinstance(at, float) else at
        return af(out, in_, AF.Sigmoid, bias, 1000.0 * sign, accum)

    def dma(q, cost, reads, writes, out, in_, slow=False):
        qq = {"sp": g.sync, "act": g.scalar, "pool": g}[q]
        if slow:
            op(q, cost, reads, writes, lambda: qq.dma_start(out, in_, allow_slow_non_contiguous=True), "dma")
        else:
            op(q, cost, reads, writes, lambda: qq.dma_start(out, in_), "dma")

    def send(reads, writes, out, in_):
        op("pool", NET, reads, writes, lambda sem: g.remote_dma(out, in_, sem, T.sem.sent, pid, rid, mask), "send")

    def slots(b):
        return ["%s.%d" % (b, s) for s in range(4)]

    ps = {b: T["ps" + b] for b in BANKS}
    TAB = ["tab%d" % c for c in range(4)]

    dma("sp", 2.2, [], ["lin0"], T.lin[:, 0:512], T.lsr[:, 0:512])
    dma("act", 2.6, [], ["xin0"], T.xin[:, 0:1024], T.xc[:, 0:1024])
    dma("sp", 3.2, [], ["lin1"], T.lin[:, 512:1024], T.lsr[:, 512:1024])
    dma("act", 3.6, [], ["jin"], T.jin[:], T.jur[:])
    dma("sp", 4.2, [], ["xin1"], T.xin[:, 1024:2048], T.xc[:, 1024:2048])
    dma("act", 4.8, [], ["lin2"], T.lin[:, 1024:1536], T.lsr[:, 1024:1536])
    dma("sp", 5.4, [], ["lin3"], T.lin[:, 1536:2048], T.lsr[:, 1536:2048])
    dma("act", 5.6, [], ["yi00", "yi01"], T.yi[:, 0:256], T.own[:])
    dma("pool", 3.0, [], ["win"], T.win[:, 0:1], T.wgt[:], True)

    def ramp(key, out, pattern, base, mul, whole=False):
        n_el = 1
        for p in pattern:
            n_el *= p[1]
        if whole:
            op("pool", 0.13 + 2 * n_el * CYC, [], [key], lambda: g.iota(out, pattern, base, mul))
        else:
            op("pool", 0.13 + 2 * n_el * CYC, [], [key],
               lambda: g.iota(out, pattern, base, mul, allow_small_or_imprecise_dtypes=True))
    ramp("dif", T.dif[:], [[1, 128]], 0, -1)
    ramp("pi", T.pi[:, 0:1], [[0, 1]], 0, 1, True)
    ramp("gm", T.gm[:], [[1, 8], [0, 16]], 0, 0)
    ramp("zc", T.zc[:], [[1, 144]], -15, 0)
    ramp("ini1", T.ini[:], [[0, 8], [32, 16]], -160, 0)
    ramp("g4", T.g4[:], [[1, 8], [0, 4]], 0, 0)
    ramp("endi", T.endi[:], [[1, 8]], 0, 0, True)
    ramp("base0", T.base[:], [[0, 2], [128, 8]], 0, 0, True)
    for key, v in (("i4k", 4096.0), ("ib", 1.0), ("ih", 1.0), ("n2h", -2048.0)):
        dve(128, ["dif"], [key], ts(T[key][:], T.dif[:], 0.0, v, OP.is_equal, OP.mult))
    for key, v in (("nib", -1.0), ("i32", 1.0), ("n4k", -4096.0), ("n2k", -2048.0), ("ibig", 262144.0), ("i16", 16.0), ("w1", -7.0)):
        act(128, ["ib"], [key], af(T[key][:], T.ib[:], AF.Identity, 0.0, v))
    for j in range(4):
        act(128, ["ib"], ["dig%d" % j], af(T.dig[:, H * j:H * j + H], T.ib[:], AF.Identity, 0.0, 32.0 ** j / 4096))

    def lin(key, reads, out, in_, scale, bias=0.0, n_el=1):
        act(n_el, reads, [key], af(out, in_, AF.Identity, bias, scale))
    pint = lambda c: T.pj[:, c:c + 1]
    dve(1, ["pi"], ["pj0"], ts(pint(0), T.pi[:, 0:1], 4, None, OP.arith_shift_right))
    dve(1, ["pi"], ["pj1"], ts(pint(1), T.pi[:, 0:1], 15, None, OP.bitwise_and))
    PG, PK, PG16, PM, PF, PZ, P8, PW, PZ4, PU, PV = [T.pf[:, c:c + 1] for c in range(11)]
    dve(2, ["pj0", "pj1"], ["pf"], cp(T.pf[:, 0:2], T.pj[:, 0:2]))
    lin("pg16", ["pf"], PG16, PG, 16.0)
    dve(1, ["pf"], ["pm0"], ts(PW, PK, 0.0, None, OP.is_equal))
    lin("pm", ["pm0"], PM, PW, 1000.0, -500.0)
    lin("pfar", ["pf"], PF, PK, 37.0 * 32.0)
    lin("pz", ["pf"], PZ, PK, 1.0, 1.0)
    lin("p8", ["pf"], P8, PK, 8.0)
    lin("pz4", ["pf"], PZ4, PK, -4096.0, -4096.0)
    for j in range(4):
        dve(8, ["g4", "pf"], ["sj%d" % j], ts(T.sj[:, j:32:4], T.g4[:, j:32:4], PG, 32.0 ** -j, OP.is_equal, OP.mult))
    SJ = ["sj%d" % j for j in range(4)]
    dve(16, ["base0", "p8"], ["base0"], ts(T.base[:], T.base[:], P8, None, OP.add))
    dve(128, ["gm", "pf"], ["bo"], ts(T.bo[:], T.gm[:], PG, None, OP.is_equal))
    dve(144, ["zc", "pg16"], ["zs"], ts(T.zs[:], T.zc[:], PG16, None, OP.is_equal))
    lin("zt", ["zs"], T.zt[:], T.zs[:], 32.0, 0.0, 144)
    lin("g8", ["bo"], T.g8[:], T.bo[:, 0:128:16], 1.0)
    lin("g8s", ["bo"], T.g8s[:], T.bo[:, 0:128:16], 512.0)
    dve(128, ["dif"], ["tmp"], ts(T.tmp[:], T.dif[:], 0.0, None, OP.is_gt))
    dve(128, ["tmp", "bo"], ["tmp"], tt(T.tmp[:], T.tmp[:], T.bo[:], OP.mult), 2.0)
    dve(128, ["tmp", "ib"], ["tri"], tt(T.tri[:], T.ib[:], T.tmp[:], OP.subtract), 2.0)
    dve(8, ["ib", "tri"], ["tmp"], ts(T.tmp[:, 0:8], T.ib[:, 0:128:16], 17.0, None, OP.mult))
    dve(8, ["tmp", "g8"], ["tri"], tt(T.tri[:, 0:128:16], T.tmp[:, 0:8], T.g8[:], OP.subtract))
    lin("ntri", ["tri"], T.ntri[:], T.tri[:], -1.0, 0.0, 128)
    dve(128, ["w1", "bo"], ["w1"], tt(T.w1[:], T.w1[:], T.bo[:], OP.add), 2.0)
    dve(128, ["i16", "bo"], ["w2"], tt(T.w2[:], T.i16[:], T.bo[:], OP.add), 2.0)
    lin("wz32", ["bo", "pz"], T.wz32[:], T.bo[:], PZ, 0.0, 128)
    lin("wz4", ["bo", "pz4"], T.wz4[:], T.bo[:], PZ4, 0.0, 128)
    if CFG["yz"] == "inc":
        dve(128, ["wz32"], ["wz"], cp(T.wz[:], T.wz32[:]))
    else:
        lin("nwz", ["wz32"], T.nwz[:], T.wz32[:], -1.0, 0.0, 128)
    dve(8, ["endi"], ["ends"], cp(T.ends[:], T.endi[:]))
    for c, b in enumerate(("C0", "C1", "D0", "D1")):
        calls = []
        for j in range(4):
            k = 4 * c + j
            calls += group(ps[b][:, H * j:H * j + H], [(T.ib[:], T.zt[:, 15 - k:143 - k]), (T.ib[:], T.ib[:])])
        mm(["ib", "zt"], slots(b), calls)
        act(512, slots(b), ["wf%d" % c], af(T.wf[:, 512 * c:512 * c + 512], ps[b][:], AF.Identity))
    WFK = ["wf%d" % c for c in range(4)]

    def fill(key, ap, v, n_el, after=()):
        dve(n_el, list(after), [key], lambda: ve.memset(ap, v), 0.5)
    fill("c160", T.c160[:], 160.0, 512)
    fill("cw", T.cw[:], -5.15625, 128)
    for k in range(8):
        fill("cw", T.cw[:, k:128:16], -5.0 * (k // 4), 8, ["cw"])
    fill("cu", T.cu[:], 1.0, 128)
    dve(1, ["pf"], ["pu"], ts(PU, PK, 0.0, 2048.0 * 1024, OP.is_equal, OP.mult))
    dve(1, ["pf"], ["pv"], ts(PV, PK, 1.0, 2080.0, OP.is_equal, OP.mult))
    dve(1, ["pu", "pv"], ["pu"], tt(PU, PU, PV, OP.add))
    lin("wu", ["bo", "pu"], T.wu[:], T.bo[:], PU, 0.0, 128)
    fill("rst", T.rst[:], -1.0e6, 256)
    fill("rst", T.rst[:, 0:128:16], 131072.0, 8, ["rst"])
    fill("o16", T.o16[:], 0.0625, 256)
    fill("thr", T.thr[:, 0:1], -4500.0, 1)
    WF, WLO, W7 = T.wcol[:, 0:1], T.wcol[:, 1:2], T.wcol[:, 2:3]
    dve(1, ["win"], ["wf"], cp(WF, T.win[:, 0:1]))
    dve(1, ["wf"], ["whi"], cp(T.wcb[:, 0:1], WF))
    dve(1, ["wf", "whi"], ["wlo"], tt(WLO, WF, T.wcb[:, 0:1], OP.subtract))
    dve(1, ["win"], ["w7i"], ts(T.win[:, 4:5], T.win[:, 0:1], 7, None, OP.bitwise_and))
    dve(1, ["w7i"], ["w7"], cp(W7, T.win[:, 4:5]))
    lin("wh", ["bo", "wf"], T.wh[:], T.bo[:], WF, 0.0, 128)
    lin("wl", ["bo", "wlo"], T.wl[:], T.bo[:], WLO, 0.0, 128)
    lin("zw", ["zs", "w7"], T.zw[:], T.zs[:], W7, 0.0, 144)
    dve(256, ["jin"], ["ui00", "ui01"], cp(T.ui[:, 0:256], T.jin[:]))
    for c, b in enumerate(("A0", "A1", "B0", "B1")):
        s = slice(512 * c, 512 * c + 512)
        mm(["i4k", "xin%d" % (c // 2)], slots(b), group(ps[b][:], [(T.i4k[:], T.xin[:, s])], True, 512))
        dve(512, slots(b) + ["lin%d" % c], ["tab%d" % c], tt(T.tab[:, s], T.lin[:, s], ps[b][:], OP.add))
    if CFG["yz"] == "inc":
        for c, b in enumerate(("C0", "D0", "C1", "D1")):
            s = slice(512 * c, 512 * c + 512)
            mm(["tab%d" % c, "xin%d" % (c // 2), "wz4", "wz32"], slots(b),
               [(ps[b][:], T.wz4[:], T.xin[:, s], True, False, 512), (ps[b][:], T.wz32[:], T.tab[:, s], False, True, 2048)])
            act(512, slots(b), ["yzt%d" % c], af(T.yzt[:, s], ps[b][:], AF.Identity))

    CX, CD, CM, CK = 1.5 * 2 ** 37, 1.5 * 2 ** 25, 1.5 * 2 ** 26, 1.5 * 2 ** 28

    def half(t, h):
        last = t == V - 1
        k_ = lambda s: "%s_%d" % (s, h)
        c = slice(H * h, H * h + H)
        A, B = "A%d" % h, "B%d" % h
        sl = lambda b, s: ps[b][:, H * s:H * s + H]

        def at(name):
            p = CFG["at"][name]
            b = p[0] + (p[2] if len(p) > 2 else "%d" % h)
            return b, H * int(p[1]), "%s.%s" % (b, p[1])
        pa = lambda name: ps[at(name)[0]][:, at(name)[1]:at(name)[1] + H]
        pk = lambda name: at(name)[2]
        byk = lambda name, k, s: ps[at(name)[0]][:, at(name)[1] + k:at(name)[1] + H:s]
        o0 = 256 * t + H * h
        o1 = o0 + 256
        Y, U, YN = T.yi[:, o0:o0 + H], T.ui[:, o0:o0 + H], T.yq[:, o0:o0 + H]
        ky, ku, kyn = "yi%d%d" % (t, h), "ui%d%d" % (t, h), "yq%d%d" % (t, h)
        q0 = 2048 * h
        ch = lambda buf, q, w=1: buf[:, q0 + 512 * q:q0 + 512 * (q + w)]
        kk = lambda buf, s: buf[:, q0 + H * s:q0 + H * (s + 1)]
        gj = lambda buf, k: buf[:, q0 + k:q0 + 2048:16]
        jur = lambda s: s // 4 + 4 * (s % 4)
        gk = []
        for e, i0, i1 in CFG["gx"][h]:
            src = T.tab[:, 0:2048].indirect(T.ui[:, o0 + i0:o0 + i1])
            out = T.gg[:, q0 + 16 * i0:q0 + 16 * i1]
            gk.append(k_("g%d" % i0))
            if e == "act":
                act(16 * (i1 - i0), TAB + [ku], gk[-1:], af(out, src, AF.Identity), GC)
            else:
                dve(16 * (i1 - i0), TAB + [ku], gk[-1:], cp(out, src), GC)
        mm(["i4k", "n4k", "c160", ky], [pk("y")], group(pa("y"), [(T.n4k[:], T.c160[:, 0:H]), (T.i4k[:], Y)]))
        dve(H, [ku], [k_("r16")], cp(T.r16[:, c], U), 0.5)
        for q in range(4):
            dve(H, gk + [pk("y")], [k_("d%d" % q)],
                many([tt(kk(T.d, s), gj(T.gg, jur(s)), pa("y"), OP.subtract) for s in range(4 * q, 4 * q + 4)]), 1.0, 4)
        pick = lambda k, whole: (byk("nom", k, 16), gj(T.gg, k), T.i32[:, (k + t) % 16:128:16], whole, whole or k == 15, 256)
        if CFG["nom"] == 1:
            for q in range(4):
                mm(gk + ["i32"], [pk("nom")], [pick(k, True) for k in range(4 * q, 4 * q + 4)])
            act(H, [pk("nom")], [k_("n32")], af(T.n32[:, c], pa("nom"), AF.Identity))
            act(H, [pk("nom")], [k_("nr")], af(T.nr[:, c], pa("nom"), AF.Identity, 160.0, 1.0 / 4096))
            mm([k_("n32"), k_("nr"), "i32", "n4k"], [pk("nt")],
               [(pa("nt"), T.nr[:, c], T.n4k[:], True, False, 128), (pa("nt"), T.n32[:, c], T.i32[:], False, True, 512)])
            dve(H, [pk("nt")], [k_("nu")], ts(T.nu[:, c], pa("nt"), 160.0 * 4096, None, OP.add))
            dve(H, [k_("nu")], [k_("n16")], ts(T.n16[:, c], T.nu[:, c], -2048.0, None, OP.add), 0.5)
            n16 = (T.ih[:], T.n16[:, c])
        else:
            mm(["i4k", "c160"], [pk("nom")], group(pa("nom"), [(T.i4k[:], T.c160[:, 0:H])], True, 128, False))
            for q in range(4):
                mm(gk + ["i32", pk("nom")], [pk("nom")], [pick(k, False) for k in range(4 * q, 4 * q + 4)])
            act(H, [pk("nom")], [k_("nr")], af(T.nr[:, c], pa("nom"), AF.Identity, 0.0, 1.0 / 4096))
            mm([k_("nr"), "n4k", pk("nom")], [pk("nom")], group(pa("nom"), [(T.n4k[:], T.nr[:, c])], False))
            dve(H, [pk("nom")], [k_("n16")], ts(T.n16[:, c], pa("nom"), -2048.0, None, OP.add))
            n16 = (T.n16[:, c], T.ih[:])
            mm([k_("n16"), "ih"], [pk("nt")], group(pa("nt"), [n16]))
            dve(H, [pk("nt")], [k_("nu")], ts(T.nu[:, c], pa("nt"), 2048.0, None, OP.add))
        zk = []
        for e, i0, i1 in CFG["gz"][h]:
            src = T.tab[:, 0:2048].indirect(T.nu[:, H * h + i0:H * h + i1])
            out = T.zz[:, q0 + 16 * i0:q0 + 16 * i1]
            zk.append(k_("z%d" % i0))
            if e == "act":
                act(16 * (i1 - i0), TAB + [k_("nu")], zk[-1:], af(out, src, AF.Identity, 160.0, 1.0 / 4096), GC)
            else:
                dve(16 * (i1 - i0), TAB + [k_("nu")], zk[-1:], ts(out, src, 1.0 / 4096, 160.0, OP.mult, OP.add), GC)
        for q in range(4):
            mm([k_("d%d" % q)] + ["dig%d" % j for j in range(4)], ["%s.%d" % (A, q)],
               group(sl(A, q), [(T.dig[:, H * j:H * j + H], kk(T.d, 4 * q + j)) for j in range(4)]))
        mm(["ib", "ini1"], [pk("key")], group(pa("key"), [(T.ib[:], T.ini[:])], True, 128, False))
        for q in (0, 2):
            dk = [k_("d%d" % q), k_("d%d" % (q + 1))]
            dve(1024, dk, [k_("fx%d" % q)], ts(ch(T.fx, q, 2), ch(T.d, q, 2), CX - 160.0 * 4096, CX, OP.add, OP.not_equal), 0.5)
            act(1024, dk, [k_("ad%d" % q)], af(ch(T.ad, q, 2), ch(T.d, q, 2), AF.Abs, -160.0, 1.0 / 4096))
            mm([k_("ad%d" % q), "g8s", pk("key")], [pk("key")],
               [(byk("key", jur(s), 16), kk(T.ad, s), T.g8s[:], False, False, 64) for s in range(4 * q, 4 * q + 8)])
        for q in (0, 2):
            mm([k_("fx%d" % q)] + WFK + ([pk("v")] if q else []), [pk("v")],
               group(pa("v"), [(T.wf[:, H * jur(s):H * jur(s) + H], kk(T.fx, s)) for s in range(4 * q, 4 * q + 8)], q == 0, 128, q == 2))
        act(H, [pk("v")], [k_("bad")], af(T.bad[:, c], pa("v"), AF.Identity, 128.0 + 15.0 / 64, 1.0 / 32))
        act(H, [pk("v")], [k_("pc")], af(T.pc[:, c], pa("v"), AF.Identity, 127.75, 1.0 / 32))
        act(H, [pk("v")], [k_("a")], step(T.a[:, c], pa("v"), 152.0, -1.0))
        mm([k_("bad"), k_("pc"), "tri", "ntri"], [pk("tri")], group(pa("tri"), [(T.tri[:], T.bad[:, c]), (T.ntri[:], T.pc[:, c])]))
        act(H, [pk("tri"), "pm"], [k_("m")], step(T.m[:, c], pa("tri"), PM))
        mm([k_("a"), "bo"], [pk("c")], group(pa("c"), [(T.bo[:], T.a[:, c])]))
        act(H, [pk("c"), "thr"], [k_("nl"), k_("acc")],
            step(T.nl[:, c], pa("c"), T.thr[:, 0:1], 1.0, None if last else T.acc[:, 4 * h:4 * h + 1]))
        mm([k_("a"), k_("nl"), "ibig", pk("key")], [pk("key")],
           group(pa("key"), [(T.a[:, c], T.ibig[:]), (T.nl[:, c], T.ibig[:])], False, 128, False))
        tq = lambda q: T.tp[:, 512 * h + H * q:512 * h + H * (q + 1)]
        for q in (0, 2):
            dve(H, [k_("m"), "%s.%d" % (A, q), "%s.%d" % (A, q + 1)], [k_("tp%d" % q)],
                many([tt(tq(j), T.m[:, c], sl(A, j), OP.mult) for j in (q, q + 1)]), 1.0, 2)
            calls = [(byk("dr", j, 4), tq(j), T.sj[:], False, j == 3, 256) for j in (q, q + 1)]
            if q == 0:
                calls = [(pa("dr"), T.ib[:], T.cw[:], True, False, 128)] + calls
            mm([k_("tp%d" % q), "ib", "cw"] + SJ + ([pk("dr")] if q else []), [pk("dr")], calls)
        dve(H, [pk("dr")], [k_("ra")], ts(T.ra[:, c], pa("dr"), CK, -CK - 160.0, OP.add, OP.add))
        dve(H, [pk("dr"), k_("ra")], [k_("dr")], tt(T.dr[:, c], T.ra[:, c], pa("dr"), OP.subtract))
        mm([k_("dr"), "nib", pk("key")], [pk("key")], group(pa("key"), [(T.nib[:], T.dr[:, c])], False))
        dve(H, [k_("dr")], [k_("fo")], ts(T.fo[:, c], T.dr[:, c], CD + 160.0, CD, OP.add, OP.not_equal), 0.5)
        dve(H, [pk("key"), "rst"], [k_("mins")],
            lambda: ve.tensor_tensor_scan(T.mins[:, c], T.rst[:], pa("key"), 131072.0, OP.max, OP.min))
        me, rb, db = T.mins[:, H * h + 15:H * h + H:16], T.rb[:, 8 * h:8 * h + 8], T.db[:, 16 * h:16 * h + 8]
        dve(8, [k_("mins")], [k_("rb")], ts(rb, me, CK, -CK, OP.add, OP.add))
        dve(8, [k_("mins"), k_("rb")], [k_("db")], tt(db, me, rb, OP.subtract))
        dve(H, [k_("db"), "ends"], [k_("dbc")], cp(T.dbc[:, c], db.indirect(T.ends[:])), GC)
        mm([k_("dbc"), "ib"], [pk("dl")], group(pa("dl"), [(T.dbc[:, c], T.ib[:])]))
        mm([k_("dbc"), k_("dr"), "ib"], [pk("dn")], group(pa("dn"), [(T.ib[:], T.dr[:, c]), (T.ib[:], T.dbc[:, c])]))
        dve(H, [pk("dl"), k_("m")], [pk("dl")], tt(pa("dl"), T.m[:, c], pa("dl"), OP.mult))
        dve(H, [pk("dl"), ky], [kyn], tt(YN, Y, pa("dl"), OP.add))
        send([kyn], ["yi%d%d" % (t + 1, h)], T.yi[:, o1:o1 + H], YN)
        dve(H, [pk("dn")], [k_("fn")], ts(T.fn[:, c], pa("dn"), CD + 160.0, CD, OP.add, OP.not_equal))
        mm([k_("fn"), k_("fo"), k_("pc"), "ib", "nib"], [pk("a2")],
           group(pa("a2"), [(T.ib[:], T.pc[:, c]), (T.fo[:, c], T.nib[:]), (T.fn[:, c], T.ib[:])]))
        act(H, [pk("a2")], [k_("a2")], step(T.a2[:, c], pa("a2"), 132.5, -1.0))
        mm([k_("a2"), "w2"], [pk("w2")], group(pa("w2"), [(T.w2[:], T.a2[:, c])]))
        act(H, [pk("w2")], [k_("wa")], step(T.wa[:, c], pa("w2"), 27.5))
        mm([k_("a2"), "w1"], [pk("w1")], group(pa("w1"), [(T.w1[:], T.a2[:, c])]))
        dve(H, [pk("w1")], [k_("m1")], ts(T.m1[:, c], pa("w1"), CM, CM + 8.0, OP.add, OP.not_equal))
        if "dve" in CFG["zs"][h]:
            mm([kyn, "ib"], [pk("yn")], group(pa("yn"), [(T.ib[:], YN)]))
        mm([kyn, "wh", "wl"], [pk("u")], group(pa("u"), [(T.wh[:], YN), (T.wl[:], YN)]))
        dve(H, [pk("u")], [k_("ur")], ts(T.ur[:, c], pa("u"), 1.0 / 2048, 1024.5 + 2.0 ** -12, OP.mult, OP.add))
        mm([kyn, "wh", "wl", "wu", "cu", "n2h", k_("ur")], [pk("u")],
           group(pa("u"), [(T.wh[:], YN), (T.wl[:], YN), (T.wu[:], T.cu[:]), (T.n2h[:], T.ur[:, c])]))
        dve(H, [pk("u"), k_("r16")], [k_("pp")], tt(T.pp[:, c], T.r16[:, c], pa("u"), OP.mult))
        dve(H, [k_("pp"), "pfar"], [k_("pq")], ts(T.pq[:, c], T.pp[:, c], PF, None, OP.add))
        dve(H, [k_("pq")], [k_("far")], ts(T.far[:, c], T.pq[:, c], 5, 2047, OP.arith_shift_right, OP.bitwise_and))
        if h == 1:
            b, c0, key = at("col")
            w = ps[b][:, c0:c0 + 16]
            mm(["yq%d0" % t, kyn, "zw"], [key],
               group(w, [(T.zw[:, 15 - j:143 - j], T.yq[:, 256 * t + j:256 * t + 256:16]) for j in range(16)], True, 64))
            dve(16, [key], ["ca"], cp(T.ca[:], w))
            dve(16, ["ca"], ["cb"], ts(T.cb[:], T.ca[:], 7, None, OP.bitwise_and))
            dve(16, ["cb", "base0"], ["cc"], tt(T.cc[:], T.cb[:], T.base[:], OP.add))
            dve(16, ["cc"], ["col"], cp(T.col[:], T.cc[:]))
        mm([k_("n16"), k_("m1"), "ih", "i4k"], [pk("p1")], group(pa("p1"), [n16, (T.i4k[:], T.m1[:, c])]))
        dve(H, [pk("p1"), k_("r16")], [k_("t1")], tt(T.t1[:, c], T.r16[:, c], pa("p1"), OP.min))
        turn = 0
        for q in range(4):
            if CFG["zs"][h][q] != "dve":
                b = (B, A)[turn % 2]
                turn += 1
                calls = []
                for j in range(4):
                    calls += group(sl(b, j), [(T.ib[:], gj(T.zz, 4 * q + j)), (T.nib[:], YN)])
                mm(zk + [kyn, "ib", "nib"], slots(b), calls)
                if CFG["zs"][h][q] == "pe":
                    dve(512, slots(b), [k_("fz%d" % q)], ts(ch(T.fz, q), ps[b][:], CD - 160.0, CD, OP.add, OP.not_equal))
                else:
                    act(512, slots(b), [k_("dz%d" % q)], af(ch(T.dz, q), ps[b][:], AF.Abs, -160.0))
                    dve(512, [k_("dz%d" % q)], [k_("fz%d" % q)], ts(ch(T.fz, q), ch(T.dz, q), 2.5, None, OP.is_gt), 0.5)
            else:
                dve(H, zk + [pk("yn")], [k_("dz%d" % q)],
                    many([tt(kk(T.dz, k), gj(T.zz, k), pa("yn"), OP.subtract) for k in range(4 * q, 4 * q + 4)]), 1.0, 4)
                dve(512, [k_("dz%d" % q)], [k_("fz%d" % q)], ts(ch(T.fz, q), ch(T.dz, q), CD - 160.0, CD, OP.add, OP.not_equal), 0.5)
        mm([k_("wa"), "i16"], [pk("tf")], group(pa("tf"), [(T.wa[:, c], T.i16[:])], True, 128, False))
        for q in range(4):
            mm([k_("fz%d" % q), "g8", pk("tf")], [pk("tf")],
               [(byk("tf", k, 16), kk(T.fz, k), T.g8[:], False, k == 15, 64) for k in range(4 * q, 4 * q + 4)])
        act(H, [pk("tf")], [k_("tf")], step(T.tf[:, c], pa("tf"), 20.5))
        mm([k_("t1"), k_("m1"), k_("tf"), "ih", "n2k", "i4k"], [pk("p2")],
           group(pa("p2"), [(T.ih[:], T.t1[:, c]), (T.n2k[:], T.m1[:, c]), (T.tf[:, c], T.i4k[:])]))
        if not last:
            kuq = "uq%d%d" % (t, h)
            dve(H, [pk("p2"), k_("far")], [k_("t2")], tt(T.t2[:, c], T.far[:, c], pa("p2"), OP.min))
            mm([kyn, k_("tf"), "i4k", "n2k"], [pk("cn")], group(pa("cn"), [(T.i4k[:], YN), (T.tf[:, c], T.n2k[:])]))
            act(H, [pk("cn")], [k_("cn")], af(T.cn[:, c], pa("cn"), AF.Identity, 2048.0))
            mm([k_("t2"), k_("tf"), "n2k", "i32"], [pk("uq")],
               [(pa("uq"), T.tf[:, c], T.n2k[:], True, False, 128), (pa("uq"), T.i32[:], T.t2[:, c], False, True, 512)])
            dve(H, [pk("uq")], [kuq], ts(T.uq[:, o0:o0 + H], pa("uq"), 2048.0, None, OP.add))
            send([kuq], ["ui%d%d" % (t + 1, h)], T.ui[:, o1:o1 + H], T.uq[:, o0:o0 + H])
            if CFG["yz"] == "inc":
                dve(H, [kuq], [k_("w16")], cp(T.w16[:, c], T.uq[:, o0:o0 + H]), 0.5)
                mm([k_("w16"), "wz"], [pk("yz")], group(pa("yz"), [(T.wz[:], T.w16[:, c])]))
                act(H, [pk("yz")], [k_("sy")], af(T.sy[:, c], pa("yz"), AF.Identity))
        else:
            dve(H, [pk("p2"), k_("far")], [k_("t2")], tt(T.t2h[:, c], T.far[:, c], pa("p2"), OP.min))
            mm([k_("t2"), k_("tf"), "n2k", "ih"], [pk("uq")], group(pa("uq"), [(T.tf[:, c], T.n2k[:]), (T.ih[:], T.t2h[:, c])]))
            act(H, [pk("uq")], [k_("rq")], af(T.rq[:, c], pa("uq"), AF.Identity, 2048.0))
            send([k_("rq")], [k_("ri")], T.ri[:, c], T.rq[:, c])
            mm([k_("rq"), "wz32"], [pk("yz")], group(pa("yz"), [(T.wz32[:], T.rq[:, c])], True, 512))
            act(H, [pk("yz")], [k_("sy")], af(T.sy[:, c], pa("yz"), AF.Identity))

    def sums(q, b):
        s = slice(512 * q, 512 * q + 512)
        if CFG["hx"][q] == "act":
            act(512, TAB, ["hx%d" % q], af(T.hx[:, s], T.tab[:, s], AF.Identity, 160.0, 1.0 / 4096))
            terms = [(T.wz4[:], T.hx[:, s]), (T.wz4[:], T.c160[:])]
            assert False
        else:
            dve(512, TAB, ["hx%d" % q], ts(T.hx[:, s], T.tab[:, s], 1.5 * 2 ** 35, -1.5 * 2 ** 35, OP.add, OP.add))
            terms = [(T.nwz[:], T.hx[:, s])]
        mm(TAB + ["hx%d" % q, "nwz", "wz32"], slots(b),
           group(ps[b][:], terms, True, 512, False) + [(ps[b][:], T.wz32[:], T.tab[:, s], False, True, 2048)])
        act(512, slots(b), ["yzt%d" % q], af(T.yzt[:, s], ps[b][:], AF.Identity))

    YZ = ["yzt%d" % q for q in range(4)]
    for t in range(V):
        if t == V - 1 and CFG["yz"] != "inc":
            for q in range(4):
                sums(q, ("A1", "C1")[q % 2])
        half(t, 0)
        half(t, 1)
        for h in (0, 1):
            c, w = slice(H * h, H * h + H), T.col[:, 8 * h:8 * h + 8]
            s = slice(1024 * h, 1024 * h + 1024)
            if t < V - 1:
                dve(H, ["cn_%d" % h, "t2_%d" % h, "col"], TAB[2 * h:2 * h + 2],
                    tt(T.tab[:, s].indirect(w), T.cn[:, c], T.t2[:, c], OP.add), SC)
            if t == V - 1 or CFG["yz"] == "inc":
                dve(H, ["sy_%d" % h, "col"] + YZ[2 * h:2 * h + 2], YZ[2 * h:2 * h + 2], cp(T.yzt[:, s].indirect(w), T.sy[:, c]), SC)
        if t < V - 1:
            mm(["acc_0", "acc_1", "o16"], ["A1.1"], [(ps["A1"][:, H:H + 1], T.o16[:], T.acc[:, 4 * h:4 * h + 1], h == 0, h == 1, 256)
                                                     for h in (0, 1)])
            dve(1, ["A1.1"], ["ai"], cp(T.ai[:, 0:1], ps["A1"][:, H:H + 1]))
            dve(1, ["ai"], ["aj"], ts(T.aj[:, 0:1], T.ai[:, 0:1], 1, None, OP.bitwise_and))
            dve(1, ["aj"], ["thr"], ts(T.thr[:, 0:1], T.aj[:, 0:1], -1000.0, -4500.0, OP.mult, OP.add))
    dma("sp", 2.0, ["yi40", "yi41"], [], T.yo[:], T.yi[:, 1024:1280])
    dma("sp", 2.0, YZ, [], T.yz[:], T.yzt[0:128:16, :])
    dma("sp", 2.0, ["ri_0"], [], T.yj[:, 0:H], T.ri[:, 0:H])
    dma("act", 2.0, ["ri_1"], [], T.yj[:, H:2 * H], T.ri[:, H:2 * H])
    return ops, nen


def order(ops):
    LAT = COST["lat"]
    writer, readers = {}, {}
    for i, o in enumerate(ops):
        raw = set(writer[k] for k in o["r"] if k in writer)
        oth = set()
        for k in o["w"]:
            if k in writer:
                oth.add(writer[k])
            oth.update(readers.get(k, ()))
        oth.discard(i)
        o["raw"], o["oth"] = raw, oth - raw
        for k in o["r"]:
            readers.setdefault(k, []).append(i)
        for k in o["w"]:
            writer[k] = i
            readers[k] = []
    n = len(ops)
    cost = [o["cost"] for o in ops]
    hold = [o["cost"] if o["kind"] == "c" else (0.3 if o["kind"] == "send" else 0.1) for o in ops]
    eng = [o["eng"] for o in ops]
    pred = [[(p, 0.0 if eng[p] == eng[i] and ops[p]["kind"] == "c" and (p not in o["raw"] or eng[i] == "pe") else LAT)
             for p in sorted(o["raw"] | o["oth"])] for i, o in enumerate(ops)]
    uses = [[o["eng"]] + o["banks"] for o in ops]
    back = [[] for _ in ops]
    for i in range(n):
        for p, gap in pred[i]:
            back[p].append((i, gap))

    def place(keys, before, after, turned):
        left = [len(b) for b in before]
        ready = [i for i in range(n) if left[i] == 0]
        start, free = [0.0] * n, [0.0] * n
        busy = {r: [] for u in uses for r in u}
        while ready:
            i = min(ready, key=keys.get)
            ready.remove(i)
            lead = cost[i] - hold[i] if turned else 0.0
            s, e, w = free[i] + lead, eng[i], hold[i]
            calm = False
            while not calm:
                calm = True
                for r in uses[i]:
                    lst = busy[r]
                    lo, hi = 0, len(lst)
                    while lo < hi:
                        mid = (lo + hi) // 2
                        if lst[mid][1] + LAT <= s:
                            lo = mid + 1
                        else:
                            hi = mid
                    for a, b, x in lst[lo:lo + 40]:
                        pad = 0.0 if x == e else LAT
                        if a - pad >= s + w - 1e-9:
                            if a - LAT >= s + w:
                                break
                        elif b + pad > s + 1e-9:
                            s = b + pad
                            calm = False
            for r in uses[i]:
                lst = busy[r]
                j = len(lst)
                while j > 0 and lst[j - 1][0] > s:
                    j -= 1
                lst.insert(j, (s, s + w, e))
            s -= lead
            start[i] = s
            s += cost[i]
            for x, gap in after[i]:
                left[x] -= 1
                if s + gap > free[x]:
                    free[x] = s + gap
                if left[x] == 0:
                    ready.append(x)
        return start, max(start[i] + cost[i] for i in range(n))

    if "start" not in MEMO:
        tail = [0.0] * n
        for i in range(n - 1, -1, -1):
            tail[i] = cost[i] + max([tail[x] + gap for x, gap in back[i]] or [0.0])
        first = lambda keys: {i: i - 1.0e6 if ops[i]["kind"] == "dma" and not pred[i] else keys[i] for i in range(n)}

        def tighten(now):
            late = place({i: -(now[0][i] + cost[i]) for i in range(n)}, back, pred, True)
            return place(first([-(late[0][i] + cost[i]) for i in range(n)]), pred, back, False)
        best = now = tighten(place(first([-v for v in tail]), pred, back, False))
        rng = np.random.RandomState(CFG["seed"])
        for j in range(CFG["passes"]):
            shake = rng.rand(n) * CFG["shake"]
            lo = rng.rand() * now[1] - 0.5 * CFG["span"]
            new = tighten(place(first([now[0][i] + (shake[i] if lo < now[0][i] < lo + CFG["span"] else 0.5 * CFG["shake"])
                                       for i in range(n)]), pred, back, False))
            if new[1] < now[1] + CFG["slack"]:
                now = new
            if now[1] < best[1]:
                best = now
        MEMO["start"] = best
    start, end = MEMO["start"]
    seq = sorted(range(n), key=lambda i: (start[i], i))
    bank = {}
    for i in seq:
        o = ops[i]
        o["bk"] = set(bank[b][e] for b in o["banks"] for e in bank.get(b, {}) if e != eng[i])
        for b in o["banks"]:
            bank.setdefault(b, {})[eng[i]] = i
    return seq, end


def rank_program(g, core, T, topo):
    if T.rank_of(core) is None:
        return
    ops, nen = plan(g, core, T, topo)
    seq = order(ops)[0]
    queue = {"pe": g.tensor, "act": g.scalar, "dve": g.vector, "pool": g, "sp": g.sync}
    count = {"pe": 0, "act": 0, "dve": 0, "pool": 0}
    mark, seen, top = {}, {e: {} for e in queue}, {}
    ndma = nsend = 0
    for i in seq:
        o = ops[i]
        e = o["eng"]
        need = {}
        for p in o["raw"] | o["oth"] | o["bk"]:
            po = ops[p]
            if po["kind"] == "c" and po["eng"] == e and (p not in o["raw"] or e == "pe"):
                continue
            s, v = mark[p]
            need[s] = max(need.get(s, 0), v)
        for s in sorted(need):
            if seen[e].get(s, 0) < need[s]:
                queue[e].wait_ge(T.sem[s], need[s])
                seen[e][s] = need[s]
        if o["kind"] == "c":
            count[e] += 1
            mark[i] = ("c" + e, count[e])
            o["emit"]().then_inc(T.sem["c" + e], 1)
        elif o["kind"] == "dma":
            mark[i] = ("dm%d" % ndma, 16)
            ndma += 1
            o["emit"]().then_inc(T.sem[mark[i][0]], 16)
        else:
            mark[i] = ("ar%d" % nsend, nen)
            nsend += 1
            o["emit"](T.sem[mark[i][0]])
        top[mark[i][0]] = mark[i][1]
    top["sent"] = nsend * nen
    for s in sorted(top):
        g.wait_ge(T.sem[s], top[s])
